import numpy as np, ml_dtypes
CORES = [13,21,141,149]
N = 4
import mx_ref
BF = ml_dtypes.bfloat16
def entries(a):
    return np.ascontiguousarray(a.T).reshape(-1)
def table(e):
    return np.ascontiguousarray(np.reshape(e, (-1, 16)).T).astype(np.int32)
def cols(t, e):
    v = np.concatenate([t.reshape(128, -1, 4), np.zeros((128, 1, 4), BF)], axis=1)
    return np.ascontiguousarray(v[:, e]).reshape(128, -1)
def cut(t, i, w=512):
    return t[:, w * i:w * i + w]
def f(rng, *shape):
    return mx_ref.flush((rng.standard_normal(shape, dtype=np.float32) * np.exp2(rng.integers(-2, 3, shape[:-1] + (1,)))).astype(BF))
def wide(rng, *shape, cols=0):
    v = rng.standard_normal(shape, dtype=np.float32) * np.exp2(rng.integers(-12, 13, shape)).astype(np.float32)
    if cols: v *= np.repeat(np.exp2(rng.integers(-cols, cols + 1, shape[:-2] + (1, shape[-1] // 4))) * (rng.random(shape[:-2] + (1, shape[-1] // 4)) > 0.0625), 4, axis=-1).astype(np.float32)
    return mx_ref.flush(v.astype(BF))
T, V, M, CAPP, R, O = 256, 128, 192, 48, 3, 1
START = np.repeat(np.arange(N), V)
def loose(rng, at, to, who, but=-1):
    to = to.copy(); n = np.zeros((N, N), int); np.add.at(n, (at, to), 1)
    for i in rng.permutation(who):
        q = rng.integers(0, N)
        if q != but and n[:, q].sum() < M and (q == at[i] or n[at[i], q] < CAPP): n[at[i], to[i]] -= 1; n[at[i], q] += 1; to[i] = q
    return to
def turn(rng, at):
    to = at.copy(); far = 1 + rng.permutation(N - 1)
    for s in range(N):
        k = rng.permutation(np.flatnonzero(at == s))
        for i in range(min(N - 1, len(k) // CAPP)): to[k[CAPP * i:CAPP * i + CAPP]] = (s + far[i]) % N
    return to
def collect(rng, at, e):
    to = at.copy(); k = rng.permutation(np.flatnonzero(at == e))[M - (N - 1) * CAPP:]
    to[k] = (e + 1 + np.arange(len(k)) % (N - 1)) % N
    for s in range(N):
        if s != e: to[rng.permutation(np.flatnonzero(at == s))[:CAPP]] = e
    return to
def spill(rng, at, to, who, ranks):
    to = to.copy(); n = np.zeros((N, N), int); others = np.setdiff1d(np.arange(N * V), who); np.add.at(n, (at[others], to[others]), 1)
    for i in rng.permutation(who):
        q = ranks[np.argmin(np.where(n[at[i], ranks] < CAPP, n[:, ranks].sum(axis=0), N * V))]
        n[at[i], q] += 1; to[i] = q
    return to
def lists(rng, a, share=0.25):
    nx = rng.integers(0, N * T, (N, 2 * T)); free = [list(rng.permutation(2 * T)) for r in range(N)]
    way = np.zeros((R - 1, N * V), int)
    for k in range(R - 2, -1, -1):
        goal = a[k + 1] if k == R - 2 else a[k + 1] * T + way[k + 1] // 2
        known = {}
        for i in rng.permutation(N * V):
            s = int(a[k][i]); L = known.setdefault((s, int(goal[i])), [])
            if not L or rng.random() >= share:
                L.append(free[s].pop()); way[k, i] = L[-1]
            else: way[k, i] = L[rng.integers(0, len(L))]
        if k < R - 2: nx[a[k], way[k]] = goal
    nx[a[R - 2], way[R - 2]] = a[R - 1] * T + rng.integers(0, T, N * V)
    st = (way[0] // 2).reshape(N, V); bt = sum((way[k] % 2) << k for k in range(R - 1)).reshape(N, V)
    return {"nx": np.stack([table(e) for e in nx]), "st": np.stack([table(e) for e in st]), "bt": np.stack([table(e) for e in bt])}
def setup_inputs(rng):
    a = [START]
    for k in range(R - 1): a.append(loose(rng, a[k], a[k], np.arange(N * V)))
    return {"x": f(rng, N, 128, 4 * T), "w": f(rng, N, 128, R * O * 512), **lists(rng, a)}
def setup_inputs_through(rng):
    h = rng.integers(1, N); a = [START, START.copy(), (START + h) % N]
    for s in range(N):
        for g, k in enumerate(np.array_split(V * s + rng.permutation(V), -(-V // CAPP))): a[1][k] = (s + g) % N
    return {**setup_inputs(rng), **lists(rng, a)}
def setup_inputs_far(rng):
    a = [START]
    for k in range(R - 1): a.append(turn(rng, a[k]))
    a[R - 1] = loose(rng, a[R - 2], a[R - 1], np.flatnonzero(a[R - 1] == a[R - 2]))
    return {**setup_inputs(rng), **lists(rng, a)}
def setup_inputs_gather(rng):
    p = rng.permutation(N); home, end, bare = p[:3]; a = [START, START.copy()]
    for j, s in enumerate(p[2:]): a[1][rng.permutation(np.flatnonzero(START == s))[:min(CAPP, max(0, M - V - j * CAPP))]] = home
    to = collect(rng, a[1], end)
    to = spill(rng, a[1], to, np.flatnonzero(((a[1] == end) & (to != end)) | (to == bare)), np.append(p[3:], home))
    a.append(loose(rng, a[1], to, np.flatnonzero((to == a[1]) & (a[1] != end)), but=bare))
    return {**setup_inputs(rng), **lists(rng, a, share=0.75)}
def setup_inputs_stay(rng):
    p = rng.integers(0, N); a = [START, collect(rng, START, p)]
    a.append(loose(rng, a[1], a[1], np.flatnonzero(a[1] != p)))
    return {**setup_inputs(rng), **lists(rng, a)}
def setup_inputs_spread(rng):
    d = setup_inputs(rng); d["x"] = wide(rng, N, 128, 4 * T, cols=8); return d
def follow(nx, st, bt):
    n = np.concatenate([entries(t) for t in nx]); bits = np.concatenate([entries(t) for t in bt])
    at = [np.concatenate([entries(st[r]) + r * T for r in range(N)])]
    for k in range(R - 1): at.append(n[2 * at[k] + (bits >> k & 1)])
    return at
def check_inputs(d):
    b = []
    for name, top in (("nx", N * T), ("st", T), ("bt", 2 ** (R - 1))):
        if d[name].min() < 0 or d[name].max() >= top: b.append(name)
    if b: return b
    at = [t // T for t in follow(d["nx"], d["st"], d["bt"])]
    for k in range(R):
        if np.bincount(at[k], minlength=N).max() > M: b.append("walkers on a rank at step " + str(k))
    for k in range(R - 1):
        n = np.zeros((N, N), int); np.add.at(n, (at[k], at[k + 1]), 1); np.fill_diagonal(n, 0)
        if n.max() > CAPP: b.append("walkers from a rank to another from step " + str(k))
    return b
def reference(x, w, nx, st, bt):
    nodes = np.concatenate([x[r] for r in range(N)], axis=1)
    at = follow(nx, st, bt)
    y = np.zeros((N, 128, O * M), np.float32); ids = np.full((N, 2, M), -1, np.float32)
    for e in range(N):
        m = np.flatnonzero(at[R - 1] // T == e)
        ids[e, 0, :len(m)] = m // V; ids[e, 1, :len(m)] = m % V
        for k in range(R):
            c = np.full(M, -1); c[:len(m)] = at[k][m]
            q = mx_ref.quantize(cols(nodes, c))
            for o in range(O): y[e][:, M * o:M * o + M] += mx_ref.matmul(mx_ref.quantize(np.ascontiguousarray(cut(w[e], k * O + o))), q)
    return {"y": y, "id": ids}

@@ -1,0 +1,449 @@
+from concourse.bass import DstId, RemoteDMATransfer
+from concourse.mybir import dt, AluOpType, ActivationFunctionType
+
+N, CAP, TX = 4, 48, 256
+LAND = 3 * CAP
+F, B, I, U = "float32", "bfloat16", "int32", "uint16"
+CODE, PLANE = "float8_e4m3fn_x4", "uint8"
+
+
+def _sb(d, *s):
+    return ("sbuf", [128] + list(s), d)
+
+
+SCRATCH = {
+    "xb": _sb(B, 1024), "wb": _sb(B, 1536),
+    "xq": _sb(CODE, 256), "xs": _sb(PLANE, 256), "cb": _sb(CODE, 400), "cbs": _sb(PLANE, 400), "wq": _sb(CODE, 384), "ws": _sb(PLANE, 384),
+    "pk1": _sb(CODE, 144), "ps1": _sb(PLANE, 144), "pk2": _sb(CODE, 288), "ps2": _sb(PLANE, 288),
+    "fc1": _sb(CODE, 48), "fs1": _sb(PLANE, 48), "fc2": _sb(CODE, 96), "fs2": _sb(PLANE, 96),
+    "fu": _sb(U, 8), "fn": ("dram", [128, 2], I), "natl": ("dram", [8, 128, 2], I),
+    "lr": _sb(CODE, 192), "lrs": _sb(PLANE, 192), "lp": _sb(CODE, 176), "lps": _sb(PLANE, 176),
+    "pi": _sb(I, 1), "ic": _sb(I, 2), "col": _sb(F, 48), "iob": _sb(F, 16), "io16": _sb(F, 16), "eq": _sb(F, 16), "eqh": _sb(F, 16),
+    "io256": _sb(B, 256), "zb": _sb(B, 512), "d01": _sb(B, 128), "offsel": _sb(U, 16), "trc": _sb(F, 16), "ac": _sb(F, 16),
+    "data0": _sb(B, 256), "data3": _sb(B, 512), "kc": _sb(F, 12, 3), "rs": _sb(F, 64),
+    "stb": _sb(I, 16), "b0": _sb(I, 8), "b1": _sb(I, 8), "sx": _sb(I, 8), "sy": _sb(I, 8), "sz": _sb(I, 8), "sw": _sb(I, 8),
+    "q1l": _sb(U, 16), "qst": _sb(U, 8), "p1w": _sb(I, 512), "nd": _sb(F, 256), "tn": _sb(F, 8, 32), "uf": _sb(F, 8),
+    "ul": _sb(U, 32), "win2": _sb(B, 2048), "gg1": _sb(B, 128), "gs1": _sb(B, 128), "tg": _sb(B, 4, 32),
+    "x1": _sb(F, 16), "y1": _sb(F, 16), "off1": _sb(U, 4),
+    "c0l": _sb(B, 128), "vs1": _sb(B, 64), "c0m": _sb(B, 64), "w1": _sb(B, 272),
+    "d1": _sb(B, 18, 16), "td1": _sb(B, 9, 32), "l1f": _sb(F, 9), "list1": _sb(U, 10),
+    "nxs": _sb(I, 32), "nxt": _sb(I, 32), "nxr": _sb(I, 16), "mk": _sb(B, 16),
+    "g2": _sb(B, 512), "s2": _sb(B, 512), "tg2": _sb(B, 16, 32),
+    "x2": _sb(F, 64), "y2": _sb(F, 64), "off2": _sb(U, 16),
+    "vown": _sb(B, 64), "vsel": _sb(B, 256), "w2": _sb(B, 400), "d2": _sb(B, 18, 16), "td2": _sb(B, 3, 3, 32),
+    "nf": _sb(F, 3, 2, 3), "list2": _sb(U, 18),
+    "nx4": _sb(I, 32), "nt4": _sb(I, 32), "r4": _sb(I, 16), "mp": _sb(B, 16), "cp4": _sb(B, 16),
+    "p3w": _sb(B, 2048), "g3": _sb(B, 512), "s3": _sb(B, 512), "tg3": _sb(B, 16, 32), "e3": _sb(F, 32), "f3": _sb(F, 32), "y3": _sb(F, 32),
+    "off3": _sb(U, 16), "val3": _sb(B, 256), "w3": _sb(B, 448),
+    "t3": _sb(B, 6, 32), "c3": _sb(B, 6, 32), "pl": _sb(B, 192), "idl": _sb(F, 192),
+    "dp": _sb(B, 24, 16), "tp": _sb(B, 12, 32), "yy": _sb(F, 12, 10),
+    "x3": _sb(F, 12, 4), "x3m": _sb(F, 48), "y4": _sb(F, 48), "q0": _sb(U, 12), "qbc": _sb(U, 24),
+    "ps": ("psum", [128, 2560], F), "aw": _sb(F, 600), "bw": _sb(F, 264), "cw": _sb(F, 264),
+    "t1": _sb(F, 192), "t2": _sb(F, 192), "yo": _sb(F, 192),
+}
+SEMAPHORES = ["sv", "su", "so", "sz", "sq", "sa", "sb", "sk", "sp", "st", "g0", "g1", "g2", "g3", "g4", "dsb", "dnx", "dns", "dn4", "dx", "dw", "dnat",
+              "dmk", "dcb", "drow", "dz", "dy", "did", "m0", "m1", "c1", "c2", "c2p", "loc", "f0", "f1", "f1c", "f1s", "f2c", "f2s"]
+
+
+def order(topo, cores, r):
+    return sorted([k for k in range(N) if k != r], key=lambda k: topo.may_write(cores[r], cores[k]))
+
+
+def forwarders(topo, src, dst):
+    near = topo.host(src) == topo.host(dst)
+    return [k for k in topo.cores_of(src) if topo.may_write(k, dst) and (topo.die(k) == topo.die(src)) == near][:2]
+
+
+def mask_of(engines):
+    return sum(1 << e for e in engines)
+
+
+def hand_on(g, core, T, topo):
+    for i, src in enumerate(T.cores):
+        for j, dst in enumerate(T.cores):
+            if i == j or topo.may_write(src, dst) or core not in forwarders(topo, src, dst):
+                continue
+            h = forwarders(topo, src, dst).index(core)
+            k = order(topo, T.cores, j).index(i)
+            rid, pid = topo.addr(dst, core)
+            e = topo.engines(core, dst)
+            s = T.sem
+            jobs = [(s.f0, 4, T.natl[2 * i + h], T.fn[:], s.m0)]
+            if h:
+                jobs += [(s.f1, 8, T.ul[:, 8 * i:8 * i + 8], T.fu[:], s.m1),
+                         (s.f1s, 8, T.cbs[:, CAP * k:CAP * k + CAP], T.fs1[:], s.c1),
+                         (s.f2s, 8, T.lrs[:, 96 * k:96 * k + 96], T.fs2[:], s.c2)]
+            else:
+                jobs += [(s.f1c, 8, T.cb[:, CAP * k:CAP * k + CAP].bitcast(dt.uint8), T.fc1[:].bitcast(dt.uint8), s.c1),
+                         (s.f2c, 8, T.lr[:, 96 * k:96 * k + 96].bitcast(dt.uint8), T.fc2[:].bitcast(dt.uint8), s.c2)]
+            for sem, n, out, in_, to in jobs:
+                g.wait_ge(sem, n)
+                g.remote_dma(out, in_, to, s.loc, pid, rid, mask_of(e))
+            g.wait_ge(s.loc, len(jobs) * len(e))
+
+
+def rank_program(g, core, T, topo):
+    me = T.rank_of(core)
+    if me is None:
+        hand_on(g, core, T, topo)
+        return
+    A, C = AluOpType, ActivationFunctionType
+    others = order(topo, T.cores, me)
+    s, v, a = T.sem, g.vector, g.scalar
+    cnt = {}
+    known = {}
+
+    def wait(q, name, sem, n):
+        if known.get((name, sem), 0) < n:
+            q.wait_ge(s[sem], n)
+            known[(name, sem)] = n
+
+    def put(q, name, chain, free, after, f, *args, **kw):
+        for sem, n in after:
+            wait(q, name, sem, n)
+        if not free:
+            wait(q, name, chain, cnt.get(chain, 0))
+        f(*args, **kw).then_inc(s[chain], 1)
+        cnt[chain] = cnt.get(chain, 0) + 1
+        return (chain, cnt[chain])
+
+    def vec(f, *args, free=False, on="sv", after=()):
+        return put(v, "v", on, free, after, f, *args)
+
+    def act(out, in_, func=C.Identity, free=False, on="sk", after=(), **kw):
+        return put(a, "a", on, free, after, a.activation, out, in_, func, **kw)
+
+    def mm(*args, free=False, after=()):
+        return put(g.tensor, "t", "st", free, after, g.tensor.matmul_mx, *args)
+
+    def ts(out, in_, s1, op0, s2=None, op1=None, **kw):
+        if op1 is None:
+            return vec(v.tensor_scalar, out, in_, s1, None, op0, **kw)
+        return vec(v.tensor_scalar, out, in_, s1, s2, op0, op1, **kw)
+
+    def tt(out, x, y, op, **kw):
+        return vec(v.tensor_tensor, out, x, y, op, **kw)
+
+    def cp(out, in_, **kw):
+        return vec(v.tensor_copy, out, in_, **kw)
+
+    def fill(out, x, free=True, on="so"):
+        return vec(v.memset, out, x, free=free, on=on)
+
+    def scan(out, d0, d1, init, **kw):
+        return vec(v.tensor_tensor_scan, out, d0, d1, init, A.mult, A.add, **kw)
+
+    def quant(k):
+        return vec(v.quantize_mx, T.wq[:, 128 * k:128 * k + 128], T.ws[:, 128 * k:128 * k + 128], T.wb[:, 512 * k:512 * k + 512], free=True, on="sq",
+                   after=[("dw", 16)])
+
+    rest, peer = [0, 1], 2
+
+    def call(items):
+        tr = []
+        for d, n, of, sem, src, dst in items:
+            e = topo.engines(core, d)
+            h = len(e) // of
+            rid, pid = topo.addr(d, core)
+            tr.append(RemoteDMATransfer(dst_ids=[DstId(rid=rid, pnc=pid)], dma_engine_mask=mask_of(e[n * h:n * h + h]), remote_sem=sem, src=src, dst=dst))
+            cnt["loc"] = cnt.get("loc", 0) + h
+        g.remote_dma_fused(tr, local_sem=s.loc)
+
+    def to_rest(h, after, sem, src, dst):
+        wait(g, "g", *after)
+        call([(forwarders(topo, core, T.cores[others[k]])[h], k, len(rest), sem, src(k), dst) for k in rest])
+
+    def to_peer(after, sem, src, dst):
+        wait(g, "g", *after)
+        call([(T.cores[others[peer]], 0, 1, sem, src(peer), dst)])
+
+    col = {}
+
+    def new(name, n=1):
+        assert name not in col
+        at = sum(col[k][1] for k in col)
+        col[name] = (T.col[:, at:at + n], n, at)
+        return col[name][0]
+
+    def c(name):
+        return col[name][0]
+
+    def eq(r, n=1):
+        return T.eq[:, r:r + n]
+
+    g.sync.dma_start(T.natl[2 * me:2 * me + 2], T.nx[:]).then_inc(s.dnat, 16)
+    for q in range(8):
+        g.sync.dma_start(T.stb[16 * q:16 * q + 16, 0:8], T.st[:]).then_inc(s.dsb, 16)
+        a.dma_start(T.stb[16 * q:16 * q + 16, 8:16], T.bt[:]).then_inc(s.dsb, 16)
+    k = fill(T.p1w[:], 0, on="sz")
+    for q in range(4):
+        e, n = (g.sync, "s") if q % 2 else (a, "a")
+        wait(e, n, *k)
+        e.dma_start(T.p1w[32 * q:32 * q + 1, :], T.nx[:]).then_inc(s.dnx, 16)
+    kz = fill(T.zb[:], 0.0, on="sp")
+    fill(T.nxs[:], 0, free=False, on="sz")
+    k = fill(T.nx4[:], 0, on="sz")
+    wait(g.sync, "s", *k)
+    for q in range(4):
+        g.sync.dma_start(T.nxs[32 * q:32 * q + 16, :], T.nx[:]).then_inc(s.dns, 16)
+    a.dma_start(T.xb[:], T.x[:]).then_inc(s.dx, 16)
+    g.sync.dma_start(T.nx4[32 * me:32 * me + 16, :], T.nx[:]).then_inc(s.dn4, 16)
+    wait(g.sync, "s", *kz)
+    for r in range(4):
+        g.sync.dma_start(T.p3w[:, 512 * r:512 * r + 512], T.zb[:]).then_inc(s.dz, 16)
+
+    def iota(out, pattern, sem, base=0):
+        g.iota(out, pattern, base, 0, allow_small_or_imprecise_dtypes=True).then_inc(sem, 1)
+    g.iota(T.pi[:], [[0, 1]], 0, 1).then_inc(s.g0, 1)
+    iota(T.io16[:], [[1, 16]], s.g3)
+    iota(T.iob[:], [[32, 16]], s.g3)
+    iota(T.io256[:], [[1, 256]], s.g1, 1)
+    g.wait_ge(s.dnat, 16)
+    call([(forwarders(topo, core, T.cores[others[k]])[h], 2 * k + h, 2 * len(rest), s.f0, T.natl[2 * me + h], T.fn[:]) for k in rest for h in (0, 1)])
+    call([(T.cores[others[peer]], h, 2, s.m0, T.natl[2 * me + h], T.natl[2 * me + h]) for h in (0, 1)])
+
+    wait(v, "v", "g0", 1)
+    ts(T.ic[:, 0:1], T.pi[:], 15, A.bitwise_and, free=True)
+    ts(T.ic[:, 1:2], T.pi[:], 31, A.bitwise_and, free=True)
+    cp(new("q", 2), T.ic[:])
+    q16, q32 = T.col[:, 0:1], T.col[:, 1:2]
+    wait(v, "v", "g3", 2)
+    ts(T.eq[:], T.io16[:], q16, A.is_equal)
+    ts(T.eqh[:], T.io16[:], q32, A.is_equal, free=True)
+    ke = ts(new("even"), q32, 16.0, A.is_lt, free=True)
+    fill(T.rs[:], 1.0)
+    fill(T.w1[:, 128:272], 0.0)
+    ko = ts(T.offsel[:], T.iob[:], q32, A.add, on="sp")
+    fill(T.f3[:], 0.0)
+    kfill = fill(T.rs[:, 0:64:4], 0.0, free=False)
+    wait(a, "a", *ke)
+    wait(a, "a", *kz)
+    kz3 = act(new("z3"), eq(3), bias=eq(14), free=True)
+    act(new("z7"), eq(7), bias=eq(14), free=True)
+    act(new("u1"), q16, scale=48.0, bias=-193.0, free=True)
+    act(T.d01[:], T.zb[:, 0:128], bias=c("even"), free=True)
+    act(new("v", 2), eq(4, 2), bias=c("z3"))
+    act(new("vme"), eq(8), bias=c("z7"), free=True)
+    act(new("init1"), eq(7), scale=-272.0, bias=c("u1"), free=True)
+    v0 = col["v"][2]
+    for k in range(2):
+        act(T.win2[:, 512 * others[k]:512 * others[k] + 512], T.zb[:], bias=T.col[:, v0 + k:v0 + k + 1], free=k > 0)
+    wait(a, "a", "g1", 1)
+    for h in range(2):
+        kw = act(T.win2[:, 512 * me + h:512 * me + 512:2], T.io256[:], scale=eq(9), bias=c("vme"), free=True)
+
+    wait(v, "v", "dsb", 256)
+    ts(T.sx[:], T.stb[:, 0:8], 513.0, A.mult, free=True)
+    ts(T.b0[:], T.stb[:, 8:16], 32.0, A.mult, free=True)
+    kq = cp(T.qst[:], T.stb[:, 0:8], on="sp")
+    ts(T.sw[:], T.sx[:], 3, A.logical_shift_right, 511, A.bitwise_and)
+    ts(T.sy[:], T.b0[:], 32, A.bitwise_and, free=True)
+    ts(T.b1[:], T.stb[:, 8:16], 1, A.logical_shift_right, free=True, on="su")
+    tt(T.sz[:], T.sw[:], T.sy[:], A.add)
+    ts(T.win2[:, 512 * others[2]:512 * others[2] + 512], T.zb[:], eq(6), A.add, c("z3"), A.add, free=True, on="sp", after=[kz3])
+    cp(T.q1l[:, 0:16:2], T.sz[:])
+    cp(T.q1l[:, 1:16:2], T.sz[:], free=True)
+    wait(v, "v", "dnx", 64)
+    ts(T.nd[:], T.p1w[:].indirect(T.q1l[:]), 2.0, A.mult)
+    vec(v.transpose, T.tn[:], T.nd[:])
+    tt(T.uf[:], T.tn[:, :, 0], T.b1[:], A.add, after=[("su", cnt["su"])])
+    ku = cp(T.ul[:, 8 * me:8 * me + 8], T.uf[:])
+    mine = T.ul[:, 8 * me:8 * me + 8]
+    to_rest(1, ku, s.f1, lambda k: mine, T.fu[:])
+    to_peer(ku, s.m1, lambda k: mine, mine)
+    iota(T.w2[:, 256:400], [[0, 144]], s.g2)
+
+    act(T.c0l[:], T.io256[:].indirect(T.qst[:, 0:8]), C.Copy, free=True, on="sa", after=[kq])
+    kvs1 = act(T.vs1[:], T.c0l[:].indirect(T.offsel[:, 0:4]), C.Copy, on="sa", after=[ko])
+    act(new("lh1"), T.eqh[:, 0:1], bias=T.eqh[:, 1:2])
+    act(new("l1"), eq(0), bias=eq(1), free=True)
+    act(new("init2"), q16, scale=48.0, bias=-1.0, free=True)
+    act(new("nt"), eq(3), scale=-1.0, bias=1.0, free=True)
+    for k in range(3):
+        act(new("t%d" % k), eq(8), C.Copy, scale=float(CAP * k - LAND), free=True)
+    act(new("q16m"), q16, bias=-256.0, free=True)
+    act(new("b%d" % me), eq(13), C.Copy, scale=me + 1.0, free=True)
+    act(new("l2h"), T.eqh[:, 2:3], bias=c("lh1"))
+    act(new("l2"), eq(2), bias=c("l1"), free=True)
+    for k in range(3):
+        act(new("b%d" % others[k]), eq(13), scale=others[k] + 1.0, bias=c("t%d" % k), free=True)
+    act(T.trc[:], T.iob[:], scale=0.5, bias=c("q16m"), free=True)
+    act(T.c0m[:], T.vs1[:], scale=eq(8), bias=c("b%d" % me), free=True, after=[kvs1])
+    act(new("k8"), eq(8), bias=eq(14), free=True)
+    act(new("keep"), c("k8"), bias=c("l2h"))
+    act(new("nz"), c("l2"), scale=-1.0, bias=c("nt"), free=True)
+    act(T.data0[:], T.zb[:, 0:256], bias=c("keep"))
+    act(new("nz8"), eq(8), scale=-1.0, bias=c("nz"), free=True)
+    kw2 = act(T.data0[:, 0:256:128], T.zb[:, 0:2], bias=c("l2h"))
+    act(T.ac[:], T.trc[:], scale=-1.0, bias=-1.0, free=True, on="sb")
+    act(T.e3[:, 1:32:2], T.trc[:], C.Copy, free=True, on="sb")
+    act(new("kp"), T.eqh[:, 15:16], bias=c("l2"), free=True, on="sb")
+    k3 = act(T.data3[:], T.zb[:], bias=c("kp"), on="sb")
+
+    vec(v.transpose, T.nxt[:], T.nxs[:], free=True, on="su", after=[("dns", 64)])
+    kg1 = cp(T.gg1[:], T.win2[:].indirect(mine), after=[kw, ("sp", cnt["sp"])])
+    ts(T.nxr[:], T.nxt[:, 0:16], 8, A.logical_shift_right, on="su")
+    scan(T.gs1[:], T.d01[:], T.gg1[:], c("init1"))
+    for r in range(4):
+        km = ts(T.mk[32 * r:32 * r + 32, :], T.nxr[32 * r:32 * r + 32, :], float(others[r] if r < 3 else me), A.is_equal, free=r > 0, on="su")
+    vec(v.transpose, T.tg[:], T.gs1[:])
+    tt(T.x1[:], T.tg[:, :, 4:8], T.tg[:, :, 20:24], A.mult)
+    kxq = vec(v.quantize_mx, T.xq[:], T.xs[:], T.xb[:], free=True, on="sz", after=[("dx", 16)])
+    scan(T.y1[:], T.rs[:, 0:16], T.x1[:], 0.0, after=[kfill])
+    ts(T.off1[:], T.y1[:, 3:16:4], 128.0, A.add)
+    cp(T.w1[:].indirect(T.off1[:, 0:4]), T.vs1[:], after=[kvs1])
+    cp(T.d1[:, 0:18:2, :], T.w1[:, 128:272])
+    cp(T.d1[:, 1:18:2, :], T.w1[:, 128:272], free=True)
+    vec(v.transpose, T.td1[:], T.d1[:])
+    tt(T.l1f[:], T.td1[:, :, 0], T.td1[:, :, 16], A.add)
+    kl = ts(T.list1[:, 0:9], T.l1f[:], -1.0, A.add)
+    kpk = cp(T.pk1[:].bitcast(dt.uint32), T.xq[:].bitcast(dt.uint32).indirect(T.list1[:, 0:9]), after=[kxq])
+    ksc = act(T.ps1[:], T.xs[:].indirect(T.list1[:, 0:9]), C.Copy, on="sa", after=[kl, kxq])
+    at = order(topo, T.cores, others[peer]).index(me)
+    to_rest(0, kpk, s.f1c, lambda k: T.pk1[:, CAP * k:CAP * k + CAP].bitcast(dt.uint8), T.fc1[:].bitcast(dt.uint8))
+    to_rest(1, ksc, s.f1s, lambda k: T.ps1[:, CAP * k:CAP * k + CAP], T.fs1[:])
+    to_peer(kpk, s.c1, lambda k: T.pk1[:, CAP * k:CAP * k + CAP].bitcast(dt.uint8), T.cb[:, CAP * at:CAP * at + CAP].bitcast(dt.uint8))
+    to_peer(ksc, s.c1, lambda k: T.ps1[:, CAP * k:CAP * k + CAP], T.cbs[:, CAP * at:CAP * at + CAP])
+    iota(T.w3[:, 256:448], [[0, 192]], s.g4)
+    iota(T.c3[:], [[0, 192]], s.g4)
+
+    wait(g.sync, "s", *km)
+    wait(g.sync, "s", *kg1)
+    for b in range(0, 128, 32):
+        g.sync.dma_start(T.win2[b:b + 4, 512 * me:512 * me + 512], T.mk[:]).then_inc(s.dmk, 16)
+        g.sync.dma_start(T.win2[b + 16:b + 19, 512 * me:512 * me + 512], T.mk[0:96, :]).then_inc(s.dmk, 16)
+    g.sync.dma_start(T.wb[:], T.w[:]).then_inc(s.dw, 16)
+    g.sync.wait_ge(s.m0, 40)
+    for r in others:
+        g.sync.dma_start(T.nx4[32 * r:32 * r + 16, :], T.natl[2 * r:2 * r + 2]).then_inc(s.dn4, 16)
+    wait(g.sync, "s", *kxq)
+    g.sync.dma_start(T.cb[:, LAND:LAND + TX].bitcast(dt.uint8), T.xq[:].bitcast(dt.uint8)).then_inc(s.dcb, 16)
+    g.sync.dma_start(T.cbs[:, LAND:LAND + TX], T.xs[:]).then_inc(s.dcb, 16)
+    g.sync.dma_start(T.lp[:, 96:176].bitcast(dt.uint8), T.xq[:, 0:80].bitcast(dt.uint8)).then_inc(s.dcb, 16)
+    g.sync.dma_start(T.lps[:, 96:176], T.xs[:, 0:80]).then_inc(s.dcb, 16)
+
+    wait(a, "a", "m1", 24)
+    wait(a, "a", "dmk", 128)
+    kgb = act(T.g2[:, 256:512], T.win2[:].indirect(T.ul[:, 16:32]), C.Copy, on="sa")
+    wait(v, "v", "m1", 24)
+    wait(v, "v", "dmk", 128)
+    wait(v, "v", *kw2)
+    cp(T.g2[:, 0:256], T.win2[:].indirect(T.ul[:, 0:16]))
+    vec(v.transpose, T.nt4[:], T.nx4[:], free=True, on="su", after=[("dn4", 64)])
+    ksA = scan(T.s2[:, 0:256], T.data0[:], T.g2[:, 0:256], c("init2"))
+    ts(T.r4[:], T.nt4[:, 0:16], 8, A.logical_shift_right, on="su")
+    ts(T.cp4[:], T.nt4[:, 0:16], 1.0 - 256.0 * me, A.add, free=True, on="su")
+    ksB = scan(T.s2[:, 256:512], T.data0[:], T.g2[:, 256:512], T.s2[:, 255:256], after=[kgb])
+    vec(v.transpose, T.tg2[:, 0:8, :], T.s2[:, 0:256], free=True, on="sz")
+    kmp = ts(T.mp[:], T.r4[:], float(me), A.is_equal, on="su")
+    vec(v.transpose, T.tg2[:, 8:16, :], T.s2[:, 256:512], free=True, on="sz", after=[ksB])
+    quant(0)
+    for n, r in enumerate(sorted(range(4), key=lambda r: (r >= 2, r != me))):
+        kvsel = act(T.vown[:] if r == me else T.vsel[:, 64 * r:64 * r + 64], T.s2[:, 128 * r:128 * r + 128].indirect(T.offsel[:, 0:4]), free=n > 0, on="sa",
+                    after=[ksB if r >= 2 else ksA], scale=c("nz8" if r == me else "nz"), **({} if r == me else {"bias": c("b%d" % r)}))
+    tt(T.x2[:, 3:64:4], T.tg2[:, :, 3], T.trc[:], A.mult, on="sz")
+    for k in range(3):
+        tt(T.x2[:, k:64:4], T.tg2[:, :, k], T.tg2[:, :, 16 + k], A.mult, free=True, on="sz")
+    quant(1)
+    scan(T.y2[:], T.rs[:], T.x2[:], 0.0, on="sz")
+    tt(T.vsel[:, 64 * me:64 * me + 64], T.vown[:], T.c0m[:], A.add, free=True, after=[kvsel])
+    ts(T.off2[:], T.y2[:, 3:64:4], 256.0, A.add, on="sz")
+    kwq = quant(2)
+    wait(v, "v", "g2", 1)
+    cp(T.w2[:].indirect(T.off2[:, 0:16]), T.vsel[:], after=[("sz", cnt["sz"])])
+
+    wait(g.sync, "s", "dz", 64)
+    wait(g.sync, "s", *kmp)
+    for b in (0, 16):
+        g.sync.dma_start(T.p3w[b + 15:b + 16, :], T.mp[:]).then_inc(s.drow, 16)
+        g.sync.dma_start(T.p3w[b + 3:b + 4, :], T.cp4[:]).then_inc(s.drow, 16)
+        for k, r in enumerate(others):
+            g.sync.dma_start(T.p3w[b + k:b + k + 1, 512 * r:512 * r + 512], T.mp[32 * r:32 * r + 32, :]).then_inc(s.drow, 16)
+
+    for x in (T.aw, T.bw, T.cw):
+        act(x[:, 0:1], T.zb[:, 0:1], C.Copy, free=x is not T.aw, on="sb")
+    for k in range(3):
+        kkc = act(T.kc[:, :, k], T.zb[:, 0:12], bias=float([400, 496, 544][k]), free=True, on="sb")
+    wait(a, "a", "drow", 16 * 10)
+    kg3 = act(T.g3[:], T.p3w[:].indirect(T.ul[:]), C.Copy, on="sa")
+
+    cp(T.d2[:, 0:18:2, :], T.w2[:, 256:400])
+    cp(T.d2[:, 1:18:2, :], T.w2[:, 256:400], free=True)
+    vec(v.transpose, T.td2[:], T.d2[:])
+    scan(T.s3[:], T.data3[:], T.g3[:], 0.0, free=True, on="sz", after=[kg3, k3])
+    for h in range(2):
+        tt(T.nf[:, :, h, :], T.td2[:, :, :, 8 + h], T.td2[:, :, :, 24 + h], A.add, free=h > 0)
+    vec(v.transpose, T.tg3[:], T.s3[:], on="sz")
+    kl2 = ts(T.list2[:], T.nf[:], LAND - 1.0, A.add)
+    tt(T.e3[:, 0:32:2], T.tg3[:, :, 15], T.ac[:], A.add, on="sz")
+    cp(T.f3[:, 1:32:2], T.tg3[:, :, 31], free=True, on="sz")
+    wait(a, "a", "c1", 48)
+    wait(a, "a", "dcb", 64)
+    ksa = act(T.ps2[:, 0:192], T.cbs[:].indirect(T.list2[:, 0:12]), C.Copy, on="sa", after=[kl2])
+    ksb = act(T.ps2[:, 192:288], T.cbs[:].indirect(T.list2[:, 12:18]), C.Copy, on="sa")
+    wait(v, "v", "c1", 48)
+    wait(v, "v", "dcb", 64)
+    kpa = cp(T.pk2[:, 0:192].bitcast(dt.uint32), T.cb[:].bitcast(dt.uint32).indirect(T.list2[:, 0:12]))
+    scan(T.y3[:], T.f3[:], T.e3[:], 0.0, on="sz")
+    kpb = cp(T.pk2[:, 192:288].bitcast(dt.uint32), T.cb[:].bitcast(dt.uint32).indirect(T.list2[:, 12:18]), free=True, on="so")
+    ts(T.off3[:], T.y3[:, 1:32:2], 256.0, A.add, on="sz")
+    to_rest(0, kpa, s.f2c, lambda k: T.pk2[:, 96 * k:96 * k + 96].bitcast(dt.uint8), T.fc2[:].bitcast(dt.uint8))
+    to_rest(1, ksa, s.f2s, lambda k: T.ps2[:, 96 * k:96 * k + 96], T.fs2[:])
+    to_peer(kpb, s.c2p, lambda k: T.pk2[:, 96 * k:96 * k + 96].bitcast(dt.uint8), T.lp[:, 0:96].bitcast(dt.uint8))
+    to_peer(ksb, s.c2p, lambda k: T.ps2[:, 96 * k:96 * k + 96], T.lps[:, 0:96])
+
+    tt(T.val3[:], T.s3[:].indirect(T.offsel[:, 0:16]), T.vsel[:], A.add, free=True)
+    wait(v, "v", "g4", 2)
+    cp(T.w3[:].indirect(T.off3[:, 0:16]), T.val3[:], after=[("sz", cnt["sz"])])
+    cp(T.dp[:, 0:24:2, :], T.w3[:, 256:448])
+    cp(T.dp[:, 1:24:2, :], T.w3[:, 256:448], free=True)
+    vec(v.transpose, T.t3[:], T.w3[:, 256:448], free=True, on="su")
+    vec(v.transpose, T.tp[:], T.dp[:])
+    tt(T.c3[:, :, 13:15], T.t3[:, :, 13:15], T.t3[:, :, 29:31], A.add, on="su")
+    kyy = tt(T.yy[:], T.tp[:, :, 0:10], T.tp[:, :, 16:26], A.add)
+    kpl = vec(v.transpose, T.pl[:], T.c3[:], on="su")
+    cp(T.qbc[0:32, 0:12], T.yy[0:32, :, 3], free=True, on="so", after=[kyy])
+    cp(T.qbc[0:32, 12:24], T.yy[0:32, :, 9], free=True, on="so")
+    tt(T.x3[:, :, 0:3], T.yy[:, :, 0:3], T.kc[:], A.add, after=[kkc])
+    ts(T.x3[:, :, 3], T.yy[:, :, 8], float(LAND), A.add, free=True)
+    cp(T.qbc[32:64, :], T.qbc[0:32, :], on="so")
+    tt(T.x3m[:], T.x3[:], T.yy[:, :, 4:8], A.mult)
+    kqbc = cp(T.qbc[64:128, :], T.qbc[0:64, :], on="so")
+    ky4 = scan(T.y4[:], T.rs[:, 0:48], T.x3m[:], 0.0)
+    for b in range(0, 128, 32):
+        kq0 = cp(T.q0[b:b + 32, :], T.y4[0:32, 3:48:4], free=True, on="so", after=[ky4])
+
+    def w(k):
+        return T.wq[:, 128 * k:128 * k + 128], T.ws[:, 128 * k:128 * k + 128]
+    m2 = mm(T.ps[:, 1024:1280], *w(2), T.xq[:], T.xs[:], True, True, free=True, after=[kwq])
+    m1 = mm(T.ps[:, 512:768], *w(1), T.xq[:], T.xs[:], True, True)
+    wait(g.tensor, "t", "c1", 48)
+    wait(g.tensor, "t", "dcb", 64)
+    m0 = mm(T.ps[:, 0:400], *w(0), T.cb[:], T.cbs[:], True, True)
+    act(T.cw[:, 1:257], T.ps[:, 1024:1280], C.Copy, on="sb", after=[m2])
+    act(T.bw[:, 1:257], T.ps[:, 512:768], C.Copy, free=True, on="sb", after=[m1])
+    kaw = act(T.aw[:, 1:401], T.ps[:, 0:400], C.Copy, free=True, on="sb", after=[m0])
+    wait(a, "a", *kaw)
+    kt1 = act(T.t1[:], T.cw[:, 0:257].indirect(T.qbc[:, 0:12]), C.Copy, on="sa", after=[kqbc])
+    kid = act(T.idl[:], T.pl[:], bias=-1.0, on="sa", after=[kpl])
+    wait(g.sync, "s", *kid)
+    g.sync.dma_start(T.id[0:1, :], T.idl[13:14, :]).then_inc(s.did, 16)
+    g.sync.dma_start(T.id[1:2, :], T.idl[14:15, :]).then_inc(s.did, 16)
+    tt(T.t2[:], T.bw[:, 0:257].indirect(T.qbc[:, 12:24]), T.t1[:], A.add, on="so", after=[kaw, kqbc, kt1])
+
+    wait(g.tensor, "t", "c2p", 16)
+    mm(T.ps[:, 2048:2176], *w(0), T.lp[:, 0:128], T.lps[:, 0:128], True, False)
+    mp = mm(T.ps[:, 2048:2176], *w(1), T.lp[:, 48:176], T.lps[:, 48:176], False, True, free=True)
+    wait(g.tensor, "t", "c2", 32)
+    mm(T.ps[:, 1536:1680], *w(0), T.lr[:, 0:144], T.lrs[:, 0:144], True, False)
+    mr = mm(T.ps[:, 1536:1680], *w(1), T.lr[:, 48:192], T.lrs[:, 48:192], False, True, free=True)
+    kpw = act(T.aw[:, 545:593], T.ps[:, 2048:2096], C.Copy, free=True, on="sb", after=[mp])
+    cp(T.aw[:, 401:545], T.ps[:, 1536:1680], free=True, on="so", after=[mr])
+    ky = tt(T.yo[:], T.aw[:, 0:593].indirect(T.q0[:, 0:12]), T.t2[:], A.add, on="so", after=[kq0, kpw])
+    wait(g.sync, "s", *ky)
+    g.sync.dma_start(T.y[:], T.yo[:]).then_inc(s.dy, 16)
+
+    g.wait_ge(s.dy, 16)
+    g.wait_ge(s.did, 32)
+    for x in ("sv", "su", "so", "sz", "sq", "sa", "sb", "sk", "sp", "st", "loc"):
+        wait(g, "g", x, cnt[x])

@@ -1,10 +1,12 @@
 from concourse.bass import DstId, RemoteDMATransfer
 from concourse.mybir import dt, AluOpType, ActivationFunctionType
 
-N, CAP, TX = 4, 48, 256
+N, CAP, TX, M = 4, 48, 256, 192
 LAND = 3 * CAP
 F, B, I, U = "float32", "bfloat16", "int32", "uint16"
 CODE, PLANE = "float8_e4m3fn_x4", "uint8"
+ON, C1, ID0, ID1, N0, SLOT, SENT, PLACE, ENDS, C2, GOES, LEAVES = 0, 3, 4, 5, 6, 7, 10, 13, 14, 15, 17, 20
+PAIRED, TWIN = 10, 22
 
 
 def _sb(d, *s):
@@ -16,33 +18,27 @@ SCRATCH = {
     "xq": _sb(CODE, 256), "xs": _sb(PLANE, 256), "cb": _sb(CODE, 400), "cbs": _sb(PLANE, 400), "wq": _sb(CODE, 384), "ws": _sb(PLANE, 384),
     "pk1": _sb(CODE, 144), "ps1": _sb(PLANE, 144), "pk2": _sb(CODE, 288), "ps2": _sb(PLANE, 288),
     "fc1": _sb(CODE, 48), "fs1": _sb(PLANE, 48), "fc2": _sb(CODE, 96), "fs2": _sb(PLANE, 96),
-    "fu": _sb(U, 8), "fn": ("dram", [128, 2], I), "natl": ("dram", [8, 128, 2], I),
+    "fu": _sb(U, 8), "fn": ("dram", [128, 16], B), "gt": _sb(B, 64), "gl": ("dram", [3, 128, 16], B),
     "lr": _sb(CODE, 192), "lrs": _sb(PLANE, 192), "lp": _sb(CODE, 176), "lps": _sb(PLANE, 176),
-    "pi": _sb(I, 1), "ic": _sb(I, 2), "col": _sb(F, 48), "iob": _sb(F, 16), "io16": _sb(F, 16), "eq": _sb(F, 16), "eqh": _sb(F, 16),
-    "io256": _sb(B, 256), "zb": _sb(B, 512), "d01": _sb(B, 128), "offsel": _sb(U, 16), "trc": _sb(F, 16), "ac": _sb(F, 16),
-    "data0": _sb(B, 256), "data3": _sb(B, 512), "kc": _sb(F, 12, 3), "rs": _sb(F, 64),
-    "stb": _sb(I, 16), "b0": _sb(I, 8), "b1": _sb(I, 8), "sx": _sb(I, 8), "sy": _sb(I, 8), "sz": _sb(I, 8), "sw": _sb(I, 8),
-    "q1l": _sb(U, 16), "qst": _sb(U, 8), "p1w": _sb(I, 512), "nd": _sb(F, 256), "tn": _sb(F, 8, 32), "uf": _sb(F, 8),
-    "ul": _sb(U, 32), "win2": _sb(B, 2048), "gg1": _sb(B, 128), "gs1": _sb(B, 128), "tg": _sb(B, 4, 32),
-    "x1": _sb(F, 16), "y1": _sb(F, 16), "off1": _sb(U, 4),
-    "c0l": _sb(B, 128), "vs1": _sb(B, 64), "c0m": _sb(B, 64), "w1": _sb(B, 272),
-    "d1": _sb(B, 18, 16), "td1": _sb(B, 9, 32), "l1f": _sb(F, 9), "list1": _sb(U, 10),
-    "nxs": _sb(I, 32), "nxt": _sb(I, 32), "nxr": _sb(I, 16), "mk": _sb(B, 16),
-    "g2": _sb(B, 512), "s2": _sb(B, 512), "tg2": _sb(B, 16, 32),
-    "x2": _sb(F, 64), "y2": _sb(F, 64), "off2": _sb(U, 16),
-    "vown": _sb(B, 64), "vsel": _sb(B, 256), "w2": _sb(B, 400), "d2": _sb(B, 18, 16), "td2": _sb(B, 3, 3, 32),
-    "nf": _sb(F, 3, 2, 3), "list2": _sb(U, 18),
-    "nx4": _sb(I, 32), "nt4": _sb(I, 32), "r4": _sb(I, 16), "mp": _sb(B, 16), "cp4": _sb(B, 16),
-    "p3w": _sb(B, 2048), "g3": _sb(B, 512), "s3": _sb(B, 512), "tg3": _sb(B, 16, 32), "e3": _sb(F, 32), "f3": _sb(F, 32), "y3": _sb(F, 32),
-    "off3": _sb(U, 16), "val3": _sb(B, 256), "w3": _sb(B, 448),
-    "t3": _sb(B, 6, 32), "c3": _sb(B, 6, 32), "pl": _sb(B, 192), "idl": _sb(F, 192),
-    "dp": _sb(B, 24, 16), "tp": _sb(B, 12, 32), "yy": _sb(F, 12, 10),
-    "x3": _sb(F, 12, 4), "x3m": _sb(F, 48), "y4": _sb(F, 48), "q0": _sb(U, 12), "qbc": _sb(U, 24),
-    "ps": ("psum", [128, 2560], F), "aw": _sb(F, 600), "bw": _sb(F, 264), "cw": _sb(F, 264),
+    "pmi": _sb(F, 32), "ee": _sb(F, 32), "e2": _sb(F, 10), "e16": _sb(F, 4), "col": _sb(F, 32), "io32": _sb(I, 16), "io4": _sb(F, 4),
+    "io256": _sb(B, 256), "d01": _sb(B, 128), "offsel": _sb(U, 16), "ntr": _sb(F, 16), "data0": _sb(B, 512),
+    "rs": _sb(F, 48), "rs7": _sb(F, 112), "half": _sb(B, 16), "winb": _sb(B, 16), "bs": _sb(F, 4), "bt0": _sb(F, 4),
+    "stb": _sb(I, 16), "b0": _sb(I, 8), "sx": _sb(I, 8), "sy": _sb(I, 8), "sz": _sb(I, 8), "sw": _sb(I, 8),
+    "lists": _sb(U, 48), "p1w": _sb(I, 512), "b1r": _sb(B, 256), "nd": _sb(F, 256), "tn": _sb(F, 8, 32), "ul": _sb(U, 32),
+    "nxs": _sb(I, 32), "nxt": _sb(I, 32), "nxr": _sb(I, 16), "mk": _sb(B, 16), "win": _sb(B, 2048),
+    "gg1": _sb(B, 128), "gs1": _sb(B, 128), "tg": _sb(B, 4, 32), "x1": _sb(F, 16), "y1": _sb(F, 16), "off1": _sb(U, 4),
+    "vs1": _sb(B, 64), "c0m": _sb(B, 64), "w1": _sb(B, 272), "d1": _sb(B, 18, 16), "td1": _sb(B, 9, 32), "l1f": _sb(F, 9), "list1": _sb(U, 10),
+    "g2": _sb(B, 512), "s2": _sb(B, 640), "tg2": _sb(B, 16, 32), "x2": _sb(F, 112), "y2": _sb(F, 112), "off2": _sb(U, 16),
+    "vsel": _sb(B, 256), "w2": _sb(B, 848), "d2": _sb(B, 18, 16), "td2": _sb(B, 3, 3, 32), "nf": _sb(F, 3, 2, 3), "list2": _sb(U, 18),
+    "idl": _sb(F, 192), "dp": _sb(B, 24, 16), "tp": _sb(B, 12, 32), "fl": _sb(F, 12, 4), "x3": _sb(F, 12, 4), "z3": _sb(F, 12), "qz": _sb(F, 24),
+    "x3m": _sb(F, 48), "y4": _sb(F, 48), "q0": _sb(U, 12), "qbc": _sb(U, 24),
+    "ps": ("psum", [128, 2560], F), "aw": _sb(F, 552), "bw": _sb(F, 264), "cw": _sb(F, 264),
     "t1": _sb(F, 192), "t2": _sb(F, 192), "yo": _sb(F, 192),
 }
-SEMAPHORES = ["sv", "su", "so", "sz", "sq", "sa", "sb", "sk", "sp", "st", "g0", "g1", "g2", "g3", "g4", "dsb", "dnx", "dns", "dn4", "dx", "dw", "dnat",
-              "dmk", "dcb", "drow", "dz", "dy", "did", "m0", "m1", "c1", "c2", "c2p", "loc", "f0", "f1", "f1c", "f1s", "f2c", "f2s"]
+SINGLE = ["k%d" % n for n in range(24)]
+CHAINS = ["sv", "su", "so", "sz", "sq", "sc", "sd", "se", "sf", "sa", "sb", "sk", "sp", "st", "sx", "t0", "t1", "t2", "r0", "r1", "r2", "r3"] + SINGLE
+SEMAPHORES = CHAINS + ["g0", "g1", "g2", "g3", "g4", "g5", "dst", "dbt", "ds1", "dnx", "dns", "dx", "dw", "dcb", "drow", "dy", "did", "dia",
+                       "m00", "m01", "m02", "m1", "c1", "c2", "c2p", "loc", "f0", "f1", "f1c", "f1s", "f2c", "f2s"]
 
 
 def order(topo, cores, r):
@@ -68,16 +64,16 @@ def hand_on(g, core, T, topo):
             rid, pid = topo.addr(dst, core)
             e = topo.engines(core, dst)
             s = T.sem
-            jobs = [(s.f0, 4, T.natl[2 * i + h], T.fn[:], s.m0)]
             if h:
-                jobs += [(s.f1, 8, T.ul[:, 8 * i:8 * i + 8], T.fu[:], s.m1),
-                         (s.f1s, 8, T.cbs[:, CAP * k:CAP * k + CAP], T.fs1[:], s.c1),
-                         (s.f2s, 8, T.lrs[:, 96 * k:96 * k + 96], T.fs2[:], s.c2)]
+                jobs = [(s.f1s, T.cbs[:, CAP * k:CAP * k + CAP], T.fs1[:], s.c1),
+                        (s.f2s, T.lrs[:, 96 * k:96 * k + 96], T.fs2[:], s.c2)]
             else:
-                jobs += [(s.f1c, 8, T.cb[:, CAP * k:CAP * k + CAP].bitcast(dt.uint8), T.fc1[:].bitcast(dt.uint8), s.c1),
-                         (s.f2c, 8, T.lr[:, 96 * k:96 * k + 96].bitcast(dt.uint8), T.fc2[:].bitcast(dt.uint8), s.c2)]
-            for sem, n, out, in_, to in jobs:
-                g.wait_ge(sem, n)
+                jobs = [(s.f0, T.gl[k], T.fn[:], s["m0%d" % k]),
+                        (s.f1, T.ul[:, 8 * i:8 * i + 8], T.fu[:], s.m1),
+                        (s.f1c, T.cb[:, CAP * k:CAP * k + CAP].bitcast(dt.uint8), T.fc1[:].bitcast(dt.uint8), s.c1),
+                        (s.f2c, T.lr[:, 96 * k:96 * k + 96].bitcast(dt.uint8), T.fc2[:].bitcast(dt.uint8), s.c2)]
+            for sem, out, in_, to in jobs:
+                g.wait_ge(sem, len(topo.engines(src, core)) // 2)
                 g.remote_dma(out, in_, to, s.loc, pid, rid, mask_of(e))
             g.wait_ge(s.loc, len(jobs) * len(e))
 
@@ -99,12 +95,17 @@ def rank_program(g, core, T, topo):
             known[(name, sem)] = n
 
     def put(q, name, chain, free, after, f, *args, **kw):
+        if chain == "*":
+            chain = [x for x in SINGLE if x not in cnt][0]
         for sem, n in after:
             wait(q, name, sem, n)
         if not free:
             wait(q, name, chain, cnt.get(chain, 0))
         f(*args, **kw).then_inc(s[chain], 1)
         cnt[chain] = cnt.get(chain, 0) + 1
+        return (chain, cnt[chain])
+
+    def last(chain):
         return (chain, cnt[chain])
 
     def vec(f, *args, free=False, on="sv", after=()):
@@ -127,6 +128,9 @@ def rank_program(g, core, T, topo):
     def cp(out, in_, **kw):
         return vec(v.tensor_copy, out, in_, **kw)
 
+    def turn(out, in_, **kw):
+        return vec(v.transpose, out, in_, **kw)
+
     def fill(out, x, free=True, on="so"):
         return vec(v.memset, out, x, free=free, on=on)
 
@@ -134,12 +138,33 @@ def rank_program(g, core, T, topo):
         return vec(v.tensor_tensor_scan, out, d0, d1, init, A.mult, A.add, **kw)
 
     def quant(k):
-        return vec(v.quantize_mx, T.wq[:, 128 * k:128 * k + 128], T.ws[:, 128 * k:128 * k + 128], T.wb[:, 512 * k:512 * k + 512], free=True, on="sq",
+        return vec(v.quantize_mx, T.wq[:, 128 * k:128 * k + 128], T.ws[:, 128 * k:128 * k + 128], T.wb[:, 512 * k:512 * k + 512], free=True, on="*",
                    after=[("dw", 16)])
 
-    rest, peer = [0, 1], 2
+    def dma(q, out, in_, sem, after=()):
+        for x in after:
+            wait(q, "s" if q is g.sync else "a", *x)
+        q.dma_start(out, in_).then_inc(s[sem], 16)
+        cnt[sem] = cnt.get(sem, 0) + 16
 
-    def call(items):
+    def iota(out, pattern, sem, base=0, by=0):
+        g.iota(out, pattern, base, by, allow_small_or_imprecise_dtypes=True).then_inc(s[sem], 1)
+
+    def level(out, x, **kw):
+        return act(out, T.io256[:, 0:out.shape[1]], scale=0.0, bias=x, **kw)
+
+    def words(x):
+        return x.bitcast(dt.uint32)
+
+    def raw(x):
+        return x.bitcast(dt.uint8)
+
+    rest, peer = [0, 1], 2
+    at = order(topo, T.cores, others[peer]).index(me)
+
+    def call(after, items):
+        for x in after:
+            wait(g, "g", *x)
         tr = []
         for d, n, of, sem, src, dst in items:
             e = topo.engines(core, d)
@@ -149,301 +174,258 @@ def rank_program(g, core, T, topo):
             cnt["loc"] = cnt.get("loc", 0) + h
         g.remote_dma_fused(tr, local_sem=s.loc)
 
-    def to_rest(h, after, sem, src, dst):
-        wait(g, "g", *after)
-        call([(forwarders(topo, core, T.cores[others[k]])[h], k, len(rest), sem, src(k), dst) for k in rest])
+    def to_rest(after, h, sem, src, held):
+        call(after, [(forwarders(topo, core, T.cores[others[k]])[h], k, 2, sem, src(k), held) for k in rest])
 
-    def to_peer(after, sem, src, dst):
-        wait(g, "g", *after)
-        call([(T.cores[others[peer]], 0, 1, sem, src(peer), dst)])
+    def to_peer(after, sem, src, lands):
+        call(after, [(T.cores[others[peer]], 0, 1, sem, src(peer), lands)])
 
     col = {}
 
-    def new(name, n=1):
-        assert name not in col
-        at = sum(col[k][1] for k in col)
-        col[name] = (T.col[:, at:at + n], n, at)
-        return col[name][0]
+    def new(name):
+        col[name] = T.col[:, len(col):len(col) + 1]
+        return col[name]
 
     def c(name):
-        return col[name][0]
+        return col[name]
 
-    def eq(r, n=1):
-        return T.eq[:, r:r + n]
+    def e2(r):
+        return T.e2[:, r:r + 1]
 
-    g.sync.dma_start(T.natl[2 * me:2 * me + 2], T.nx[:]).then_inc(s.dnat, 16)
-    for q in range(8):
-        g.sync.dma_start(T.stb[16 * q:16 * q + 16, 0:8], T.st[:]).then_inc(s.dsb, 16)
-        a.dma_start(T.stb[16 * q:16 * q + 16, 8:16], T.bt[:]).then_inc(s.dsb, 16)
-    k = fill(T.p1w[:], 0, on="sz")
-    for q in range(4):
-        e, n = (g.sync, "s") if q % 2 else (a, "a")
-        wait(e, n, *k)
-        e.dma_start(T.p1w[32 * q:32 * q + 1, :], T.nx[:]).then_inc(s.dnx, 16)
-    kz = fill(T.zb[:], 0.0, on="sp")
-    fill(T.nxs[:], 0, free=False, on="sz")
-    k = fill(T.nx4[:], 0, on="sz")
-    wait(g.sync, "s", *k)
-    for q in range(4):
-        g.sync.dma_start(T.nxs[32 * q:32 * q + 16, :], T.nx[:]).then_inc(s.dns, 16)
-    a.dma_start(T.xb[:], T.x[:]).then_inc(s.dx, 16)
-    g.sync.dma_start(T.nx4[32 * me:32 * me + 16, :], T.nx[:]).then_inc(s.dn4, 16)
-    wait(g.sync, "s", *kz)
-    for r in range(4):
-        g.sync.dma_start(T.p3w[:, 512 * r:512 * r + 512], T.zb[:]).then_inc(s.dz, 16)
-
-    def iota(out, pattern, sem, base=0):
-        g.iota(out, pattern, base, 0, allow_small_or_imprecise_dtypes=True).then_inc(sem, 1)
-    g.iota(T.pi[:], [[0, 1]], 0, 1).then_inc(s.g0, 1)
-    iota(T.io16[:], [[1, 16]], s.g3)
-    iota(T.iob[:], [[32, 16]], s.g3)
-    iota(T.io256[:], [[1, 256]], s.g1, 1)
-    g.wait_ge(s.dnat, 16)
-    call([(forwarders(topo, core, T.cores[others[k]])[h], 2 * k + h, 2 * len(rest), s.f0, T.natl[2 * me + h], T.fn[:]) for k in rest for h in (0, 1)])
-    call([(T.cores[others[peer]], h, 2, s.m0, T.natl[2 * me + h], T.natl[2 * me + h]) for h in (0, 1)])
-
-    wait(v, "v", "g0", 1)
-    ts(T.ic[:, 0:1], T.pi[:], 15, A.bitwise_and, free=True)
-    ts(T.ic[:, 1:2], T.pi[:], 31, A.bitwise_and, free=True)
-    cp(new("q", 2), T.ic[:])
-    q16, q32 = T.col[:, 0:1], T.col[:, 1:2]
-    wait(v, "v", "g3", 2)
-    ts(T.eq[:], T.io16[:], q16, A.is_equal)
-    ts(T.eqh[:], T.io16[:], q32, A.is_equal, free=True)
-    ke = ts(new("even"), q32, 16.0, A.is_lt, free=True)
-    fill(T.rs[:], 1.0)
-    fill(T.w1[:, 128:272], 0.0)
-    ko = ts(T.offsel[:], T.iob[:], q32, A.add, on="sp")
-    fill(T.f3[:], 0.0)
-    kfill = fill(T.rs[:, 0:64:4], 0.0, free=False)
-    wait(a, "a", *ke)
-    wait(a, "a", *kz)
-    kz3 = act(new("z3"), eq(3), bias=eq(14), free=True)
-    act(new("z7"), eq(7), bias=eq(14), free=True)
-    act(new("u1"), q16, scale=48.0, bias=-193.0, free=True)
-    act(T.d01[:], T.zb[:, 0:128], bias=c("even"), free=True)
-    act(new("v", 2), eq(4, 2), bias=c("z3"))
-    act(new("vme"), eq(8), bias=c("z7"), free=True)
-    act(new("init1"), eq(7), scale=-272.0, bias=c("u1"), free=True)
-    v0 = col["v"][2]
-    for k in range(2):
-        act(T.win2[:, 512 * others[k]:512 * others[k] + 512], T.zb[:], bias=T.col[:, v0 + k:v0 + k + 1], free=k > 0)
-    wait(a, "a", "g1", 1)
-    for h in range(2):
-        kw = act(T.win2[:, 512 * me + h:512 * me + 512:2], T.io256[:], scale=eq(9), bias=c("vme"), free=True)
-
-    wait(v, "v", "dsb", 256)
-    ts(T.sx[:], T.stb[:, 0:8], 513.0, A.mult, free=True)
-    ts(T.b0[:], T.stb[:, 8:16], 32.0, A.mult, free=True)
-    kq = cp(T.qst[:], T.stb[:, 0:8], on="sp")
-    ts(T.sw[:], T.sx[:], 3, A.logical_shift_right, 511, A.bitwise_and)
-    ts(T.sy[:], T.b0[:], 32, A.bitwise_and, free=True)
-    ts(T.b1[:], T.stb[:, 8:16], 1, A.logical_shift_right, free=True, on="su")
-    tt(T.sz[:], T.sw[:], T.sy[:], A.add)
-    ts(T.win2[:, 512 * others[2]:512 * others[2] + 512], T.zb[:], eq(6), A.add, c("z3"), A.add, free=True, on="sp", after=[kz3])
-    cp(T.q1l[:, 0:16:2], T.sz[:])
-    cp(T.q1l[:, 1:16:2], T.sz[:], free=True)
-    wait(v, "v", "dnx", 64)
-    ts(T.nd[:], T.p1w[:].indirect(T.q1l[:]), 2.0, A.mult)
-    vec(v.transpose, T.tn[:], T.nd[:])
-    tt(T.uf[:], T.tn[:, :, 0], T.b1[:], A.add, after=[("su", cnt["su"])])
-    ku = cp(T.ul[:, 8 * me:8 * me + 8], T.uf[:])
+    G0, B0 = slice(0, 16), slice(0, 32)
+    q1l, btu, qsel, rk = T.lists[:, 0:16], T.lists[:, 16:32], T.lists[:, 32:36], T.lists[:, 40:48]
     mine = T.ul[:, 8 * me:8 * me + 8]
-    to_rest(1, ku, s.f1, lambda k: mine, T.fu[:])
-    to_peer(ku, s.m1, lambda k: mine, mine)
-    iota(T.w2[:, 256:400], [[0, 144]], s.g2)
 
-    act(T.c0l[:], T.io256[:].indirect(T.qst[:, 0:8]), C.Copy, free=True, on="sa", after=[kq])
-    kvs1 = act(T.vs1[:], T.c0l[:].indirect(T.offsel[:, 0:4]), C.Copy, on="sa", after=[ko])
-    act(new("lh1"), T.eqh[:, 0:1], bias=T.eqh[:, 1:2])
-    act(new("l1"), eq(0), bias=eq(1), free=True)
-    act(new("init2"), q16, scale=48.0, bias=-1.0, free=True)
-    act(new("nt"), eq(3), scale=-1.0, bias=1.0, free=True)
-    for k in range(3):
-        act(new("t%d" % k), eq(8), C.Copy, scale=float(CAP * k - LAND), free=True)
-    act(new("q16m"), q16, bias=-256.0, free=True)
-    act(new("b%d" % me), eq(13), C.Copy, scale=me + 1.0, free=True)
-    act(new("l2h"), T.eqh[:, 2:3], bias=c("lh1"))
-    act(new("l2"), eq(2), bias=c("l1"), free=True)
-    for k in range(3):
-        act(new("b%d" % others[k]), eq(13), scale=others[k] + 1.0, bias=c("t%d" % k), free=True)
-    act(T.trc[:], T.iob[:], scale=0.5, bias=c("q16m"), free=True)
-    act(T.c0m[:], T.vs1[:], scale=eq(8), bias=c("b%d" % me), free=True, after=[kvs1])
-    act(new("k8"), eq(8), bias=eq(14), free=True)
-    act(new("keep"), c("k8"), bias=c("l2h"))
-    act(new("nz"), c("l2"), scale=-1.0, bias=c("nt"), free=True)
-    act(T.data0[:], T.zb[:, 0:256], bias=c("keep"))
-    act(new("nz8"), eq(8), scale=-1.0, bias=c("nz"), free=True)
-    kw2 = act(T.data0[:, 0:256:128], T.zb[:, 0:2], bias=c("l2h"))
-    act(T.ac[:], T.trc[:], scale=-1.0, bias=-1.0, free=True, on="sb")
-    act(T.e3[:, 1:32:2], T.trc[:], C.Copy, free=True, on="sb")
-    act(new("kp"), T.eqh[:, 15:16], bias=c("l2"), free=True, on="sb")
-    k3 = act(T.data3[:], T.zb[:], bias=c("kp"), on="sb")
-
-    vec(v.transpose, T.nxt[:], T.nxs[:], free=True, on="su", after=[("dns", 64)])
-    kg1 = cp(T.gg1[:], T.win2[:].indirect(mine), after=[kw, ("sp", cnt["sp"])])
-    ts(T.nxr[:], T.nxt[:, 0:16], 8, A.logical_shift_right, on="su")
-    scan(T.gs1[:], T.d01[:], T.gg1[:], c("init1"))
-    for r in range(4):
-        km = ts(T.mk[32 * r:32 * r + 32, :], T.nxr[32 * r:32 * r + 32, :], float(others[r] if r < 3 else me), A.is_equal, free=r > 0, on="su")
-    vec(v.transpose, T.tg[:], T.gs1[:])
-    tt(T.x1[:], T.tg[:, :, 4:8], T.tg[:, :, 20:24], A.mult)
-    kxq = vec(v.quantize_mx, T.xq[:], T.xs[:], T.xb[:], free=True, on="sz", after=[("dx", 16)])
-    scan(T.y1[:], T.rs[:, 0:16], T.x1[:], 0.0, after=[kfill])
-    ts(T.off1[:], T.y1[:, 3:16:4], 128.0, A.add)
-    cp(T.w1[:].indirect(T.off1[:, 0:4]), T.vs1[:], after=[kvs1])
-    cp(T.d1[:, 0:18:2, :], T.w1[:, 128:272])
-    cp(T.d1[:, 1:18:2, :], T.w1[:, 128:272], free=True)
-    vec(v.transpose, T.td1[:], T.d1[:])
-    tt(T.l1f[:], T.td1[:, :, 0], T.td1[:, :, 16], A.add)
-    kl = ts(T.list1[:, 0:9], T.l1f[:], -1.0, A.add)
-    kpk = cp(T.pk1[:].bitcast(dt.uint32), T.xq[:].bitcast(dt.uint32).indirect(T.list1[:, 0:9]), after=[kxq])
-    ksc = act(T.ps1[:], T.xs[:].indirect(T.list1[:, 0:9]), C.Copy, on="sa", after=[kl, kxq])
-    at = order(topo, T.cores, others[peer]).index(me)
-    to_rest(0, kpk, s.f1c, lambda k: T.pk1[:, CAP * k:CAP * k + CAP].bitcast(dt.uint8), T.fc1[:].bitcast(dt.uint8))
-    to_rest(1, ksc, s.f1s, lambda k: T.ps1[:, CAP * k:CAP * k + CAP], T.fs1[:])
-    to_peer(kpk, s.c1, lambda k: T.pk1[:, CAP * k:CAP * k + CAP].bitcast(dt.uint8), T.cb[:, CAP * at:CAP * at + CAP].bitcast(dt.uint8))
-    to_peer(ksc, s.c1, lambda k: T.ps1[:, CAP * k:CAP * k + CAP], T.cbs[:, CAP * at:CAP * at + CAP])
-    iota(T.w3[:, 256:448], [[0, 192]], s.g4)
-    iota(T.c3[:], [[0, 192]], s.g4)
-
-    wait(g.sync, "s", *km)
-    wait(g.sync, "s", *kg1)
     for b in range(0, 128, 32):
-        g.sync.dma_start(T.win2[b:b + 4, 512 * me:512 * me + 512], T.mk[:]).then_inc(s.dmk, 16)
-        g.sync.dma_start(T.win2[b + 16:b + 19, 512 * me:512 * me + 512], T.mk[0:96, :]).then_inc(s.dmk, 16)
-    g.sync.dma_start(T.wb[:], T.w[:]).then_inc(s.dw, 16)
-    g.sync.wait_ge(s.m0, 40)
-    for r in others:
-        g.sync.dma_start(T.nx4[32 * r:32 * r + 16, :], T.natl[2 * r:2 * r + 2]).then_inc(s.dn4, 16)
-    wait(g.sync, "s", *kxq)
-    g.sync.dma_start(T.cb[:, LAND:LAND + TX].bitcast(dt.uint8), T.xq[:].bitcast(dt.uint8)).then_inc(s.dcb, 16)
-    g.sync.dma_start(T.cbs[:, LAND:LAND + TX], T.xs[:]).then_inc(s.dcb, 16)
-    g.sync.dma_start(T.lp[:, 96:176].bitcast(dt.uint8), T.xq[:, 0:80].bitcast(dt.uint8)).then_inc(s.dcb, 16)
-    g.sync.dma_start(T.lps[:, 96:176], T.xs[:, 0:80]).then_inc(s.dcb, 16)
+        dma(g.sync if b < 64 else a, T.nxs[b + 16:b + 32, :], T.nx[:], "dns")
+    dma(g.sync, T.stb[0:16, 0:8], T.st[:], "dst")
+    dma(a, T.stb[0:16, 8:16], T.bt[:], "dbt")
+    dma(a, T.stb[16:32, 0:7], T.st[:, 1:8], "ds1")
+    kp = fill(T.p1w[:], 0, on="*")
+    dma(g.sync, T.p1w[0:1, :], T.nx[:], "dnx", after=[kp])
+    dma(g.sync, T.xb[:], T.x[:], "dx")
+    iota(T.pmi[:], [[-1, 32]], "g0", by=1)
+    iota(T.half[:, 0:4], [[1, 2], [0, 2]], "g5")
+    iota(T.io256[:], [[1, 256]], "g2", base=1)
+    g.iota(T.io32[:], [[32, 16]], 0, 1).then_inc(s.g1, 1)
+    iota(T.io4[:], [[1, 4]], "g1", base=1)
+    iota(T.ntr[:], [[-32, 16]], "g3", base=-LAND, by=-1)
+    iota(T.x2[:, 6:112:7], [[32, 16]], "g3", base=LAND, by=1)
 
-    wait(a, "a", "m1", 24)
-    wait(a, "a", "dmk", 128)
-    kgb = act(T.g2[:, 256:512], T.win2[:].indirect(T.ul[:, 16:32]), C.Copy, on="sa")
-    wait(v, "v", "m1", 24)
-    wait(v, "v", "dmk", 128)
-    wait(v, "v", *kw2)
-    cp(T.g2[:, 0:256], T.win2[:].indirect(T.ul[:, 0:16]))
-    vec(v.transpose, T.nt4[:], T.nx4[:], free=True, on="su", after=[("dn4", 64)])
-    ksA = scan(T.s2[:, 0:256], T.data0[:], T.g2[:, 0:256], c("init2"))
-    ts(T.r4[:], T.nt4[:, 0:16], 8, A.logical_shift_right, on="su")
-    ts(T.cp4[:], T.nt4[:, 0:16], 1.0 - 256.0 * me, A.add, free=True, on="su")
-    ksB = scan(T.s2[:, 256:512], T.data0[:], T.g2[:, 256:512], T.s2[:, 255:256], after=[kgb])
-    vec(v.transpose, T.tg2[:, 0:8, :], T.s2[:, 0:256], free=True, on="sz")
-    kmp = ts(T.mp[:], T.r4[:], float(me), A.is_equal, on="su")
-    vec(v.transpose, T.tg2[:, 8:16, :], T.s2[:, 256:512], free=True, on="sz", after=[ksB])
-    quant(0)
-    for n, r in enumerate(sorted(range(4), key=lambda r: (r >= 2, r != me))):
-        kvsel = act(T.vown[:] if r == me else T.vsel[:, 64 * r:64 * r + 64], T.s2[:, 128 * r:128 * r + 128].indirect(T.offsel[:, 0:4]), free=n > 0, on="sa",
-                    after=[ksB if r >= 2 else ksA], scale=c("nz8" if r == me else "nz"), **({} if r == me else {"bias": c("b%d" % r)}))
-    tt(T.x2[:, 3:64:4], T.tg2[:, :, 3], T.trc[:], A.mult, on="sz")
+    p = T.pmi[:, 0:1]
+    ts(T.ee[:], T.pmi[:], 0.0, A.is_equal, on="sc", after=[("g0", 1)])
+    ts(new("m22"), p, float(TWIN), A.is_ge, -float(TWIN), A.mult, free=True, on="sc")
+    ts(new("even"), p, 16.0, A.is_lt, free=True, on="sc")
+    for b in range(0, 128, 32):
+        fill(T.nxs[b:b + 16, :], 0, on="su")
+    klists = fill(T.lists[:], 0, on="*")
+    tt(T.e2[:], T.ee[:, 0:PAIRED], T.ee[:, TWIN:TWIN + PAIRED], A.add, on="sc")
+    tt(T.e16[:], T.ee[:, 0:4], T.ee[:, 16:20], A.add, free=True, on="sc")
+    ke = tt(new("pp"), p, c("m22"), A.add, free=True, on="sc")
+
+    def column(e, on):
+        return ts(T.gt[64:128, 16 * e:16 * e + 16], T.nxt[64:128, 16:32], 1.0 - 256.0 * e, A.add, free=True, on=on)
+
+    def ends(e, on):
+        return ts(T.gt[0:64, 16 * e:16 * e + 16], T.nxr[0:64], float(e), A.is_equal, free=True, on=on, after=[kr])
+    turn(T.nxt[:], T.nxs[:], on="su", after=[("dns", 64)])
+    ts(T.sx[G0], T.stb[G0, 0:8], 513.0, A.mult, free=True, on="sx", after=[("dst", 16)])
+    ts(T.b0[G0], T.stb[G0, 8:16], 32.0, A.mult, free=True, on="sx", after=[("dbt", 16)])
+    cp(btu[G0, 0:16:2], T.stb[G0, 8:16], free=True, on="sp", after=[klists])
+    kr = ts(T.nxr[:], T.nxt[:, 16:32], 8, A.logical_shift_right, on="su")
+    kb = cp(btu[G0, 1:16:2], T.stb[G0, 8:16], free=True, on="sp")
+    for k in rest:
+        column(others[k], "t0")
+    for k in rest:
+        ends(others[k], "t0")
+    ts(T.sw[G0], T.sx[G0], 3, A.logical_shift_right, 511, A.bitwise_and, on="sx")
+    ts(T.sy[G0], T.b0[G0], 32, A.bitwise_and, free=True, on="sx")
+    ends(others[peer], "t1")
+    column(others[peer], "t1")
+    ts(new("le13"), c("pp"), PLACE + 0.5, A.is_lt, free=True, on="sd", after=[ke])
+    tt(T.sz[G0], T.sw[G0], T.sy[G0], A.add, on="sx")
+    kq = cp(qsel[B0], T.stb[B0, 0:8:2], free=True, on="*", after=[("ds1", 16)])
+    ts(new("keep"), c("pp"), float(ID1), A.is_ge, c("le13"), A.mult, on="sd")
+    kk = ts(new("keepr"), c("pp"), float(SLOT), A.is_ge, c("le13"), A.mult, free=True, on="sd")
+    cp(q1l[G0, 0:16:2], T.sz[G0], on="sx")
+    cp(q1l[G0, 1:16:2], T.sz[G0], free=True, on="sx")
+    kmine = fill(mine, 0, on="*")
+    wait(a, "a", *ke)
+    for r in range(N):
+        k = others.index(r) if r != me else 3
+        act(T.winb[:, r:r + 1], T.e16[:, k:k + 1], C.Copy, free=True)
+    kh = act(T.b1r[:], T.half[:, 0:4].indirect(btu), C.Copy, scale=0.5, free=True, on="*", after=[kb, ("g5", 1)])
+    act(new("u1"), p, scale=48.0, bias=-1.0, free=True)
+    act(new("vme"), e2(ID1), bias=e2(N0), free=True)
     for k in range(3):
-        tt(T.x2[:, k:64:4], T.tg2[:, :, k], T.tg2[:, :, 16 + k], A.mult, free=True, on="sz")
-    quant(1)
-    scan(T.y2[:], T.rs[:], T.x2[:], 0.0, on="sz")
-    tt(T.vsel[:, 64 * me:64 * me + 64], T.vown[:], T.c0m[:], A.add, free=True, after=[kvsel])
-    ts(T.off2[:], T.y2[:, 3:64:4], 256.0, A.add, on="sz")
-    kwq = quant(2)
-    wait(v, "v", "g2", 1)
-    cp(T.w2[:].indirect(T.off2[:, 0:16]), T.vsel[:], after=[("sz", cnt["sz"])])
-
-    wait(g.sync, "s", "dz", 64)
-    wait(g.sync, "s", *kmp)
-    for b in (0, 16):
-        g.sync.dma_start(T.p3w[b + 15:b + 16, :], T.mp[:]).then_inc(s.drow, 16)
-        g.sync.dma_start(T.p3w[b + 3:b + 4, :], T.cp4[:]).then_inc(s.drow, 16)
-        for k, r in enumerate(others):
-            g.sync.dma_start(T.p3w[b + k:b + k + 1, 512 * r:512 * r + 512], T.mp[32 * r:32 * r + 32, :]).then_inc(s.drow, 16)
-
-    for x in (T.aw, T.bw, T.cw):
-        act(x[:, 0:1], T.zb[:, 0:1], C.Copy, free=x is not T.aw, on="sb")
+        act(new("v%d" % k), e2(ON + k), bias=e2(ID1), free=True)
+    ends(me, "t2")
+    column(me, "t2")
+    tt(T.nd[:], T.p1w[:].indirect(q1l), T.b1r[:], A.add, on="sx", after=[("dnx", 16), kh])
+    to_rest([last("t0")], 0, s.f0, lambda k: T.gt[:, 16 * others[k]:16 * others[k] + 16], T.fn[:])
+    to_peer([last("t1")], s["m0%d" % at], lambda k: T.gt[:, 16 * others[k]:16 * others[k] + 16], T.gl[at])
     for k in range(3):
-        kkc = act(T.kc[:, :, k], T.zb[:, 0:12], bias=float([400, 496, 544][k]), free=True, on="sb")
-    wait(a, "a", "drow", 16 * 10)
-    kg3 = act(T.g3[:], T.p3w[:].indirect(T.ul[:]), C.Copy, on="sa")
+        ts(T.mk[32 * k:32 * k + 32], T.nxr[32 * k:32 * k + 32], float(others[k]), A.is_equal, free=True, on="t2")
+    ktn = turn(T.tn[B0], T.nd[B0], on="sx")
+    km = ts(T.mk[96:128], T.nxr[96:128], float(me), A.not_equal, free=True, on="t2")
+    fill(T.rs[:], 1.0, on="sz")
+    cp(T.off1[:], T.io32[:, 0:4], free=True, on="sz", after=[("g1", 2)])
+    ts(rk[B0], T.tn[B0, :, 0], -127.75, A.add, 1.0 / 256, A.mult, after=[ktn])
+    ku = ts(mine[B0], T.tn[B0, :, 0], 2.0, A.mult, on="sx", after=[kmine])
+    to_rest([ku], 0, s.f1, lambda k: mine, T.fu[:])
+    to_peer([ku], s.m1, lambda k: mine, mine)
 
-    cp(T.d2[:, 0:18:2, :], T.w2[:, 256:400])
-    cp(T.d2[:, 1:18:2, :], T.w2[:, 256:400], free=True)
-    vec(v.transpose, T.td2[:], T.d2[:])
-    scan(T.s3[:], T.data3[:], T.g3[:], 0.0, free=True, on="sz", after=[kg3, k3])
+    wait(a, "a", "g2", 1)
+    level(T.d01[:], c("even"), free=True)
+    kw1 = act(new("init1"), T.ee[:, 3:4], scale=-272.0, bias=c("u1"))
     for h in range(2):
-        tt(T.nf[:, :, h, :], T.td2[:, :, :, 8 + h], T.td2[:, :, :, 24 + h], A.add, free=h > 0)
-    vec(v.transpose, T.tg3[:], T.s3[:], on="sz")
-    kl2 = ts(T.list2[:], T.nf[:], LAND - 1.0, A.add)
-    tt(T.e3[:, 0:32:2], T.tg3[:, :, 15], T.ac[:], A.add, on="sz")
-    cp(T.f3[:, 1:32:2], T.tg3[:, :, 31], free=True, on="sz")
-    wait(a, "a", "c1", 48)
-    wait(a, "a", "dcb", 64)
-    ksa = act(T.ps2[:, 0:192], T.cbs[:].indirect(T.list2[:, 0:12]), C.Copy, on="sa", after=[kl2])
-    ksb = act(T.ps2[:, 192:288], T.cbs[:].indirect(T.list2[:, 12:18]), C.Copy, on="sa")
-    wait(v, "v", "c1", 48)
-    wait(v, "v", "dcb", 64)
-    kpa = cp(T.pk2[:, 0:192].bitcast(dt.uint32), T.cb[:].bitcast(dt.uint32).indirect(T.list2[:, 0:12]))
-    scan(T.y3[:], T.f3[:], T.e3[:], 0.0, on="sz")
-    kpb = cp(T.pk2[:, 192:288].bitcast(dt.uint32), T.cb[:].bitcast(dt.uint32).indirect(T.list2[:, 12:18]), free=True, on="so")
-    ts(T.off3[:], T.y3[:, 1:32:2], 256.0, A.add, on="sz")
-    to_rest(0, kpa, s.f2c, lambda k: T.pk2[:, 96 * k:96 * k + 96].bitcast(dt.uint8), T.fc2[:].bitcast(dt.uint8))
-    to_rest(1, ksa, s.f2s, lambda k: T.ps2[:, 96 * k:96 * k + 96], T.fs2[:])
-    to_peer(kpb, s.c2p, lambda k: T.pk2[:, 96 * k:96 * k + 96].bitcast(dt.uint8), T.lp[:, 0:96].bitcast(dt.uint8))
-    to_peer(ksb, s.c2p, lambda k: T.ps2[:, 96 * k:96 * k + 96], T.lps[:, 0:96])
+        kwme = act(T.win[:, 512 * me + h:512 * me + 512:2], T.io256[:], scale=e2(C1), bias=c("vme"), free=True, on="r3")
+    kvs1 = act(T.vs1[:], T.io256[:].indirect(qsel), C.Copy, free=True, on="*", after=[kq])
+    kreg = {}
+    for k in (peer, 0, 1):
+        for h in range(2):
+            kreg[k] = level(T.win[:, 512 * others[k] + 256 * h:512 * others[k] + 256 * h + 256], c("v%d" % k), free=True, on="r%d" % k)
+    act(new("keepo"), e2(N0), scale=-1.0, bias=c("keep"), free=True, on="sb", after=[kk])
+    act(new("u2"), c("pp"), scale=float(CAP), bias=-1.0 - CAP * SENT, free=True, on="sb")
+    act(T.bt0[:], T.io4[:], C.Copy, scale=e2(ID0), free=True, on="sb", after=[("g1", 2)])
+    level(T.data0[:, 0:512:128], c("keepr"), free=True, on="sb")
+    for r in others:
+        level(T.data0[:, 128 * r + 1:128 * r + 128], c("keep"), free=True, on="sb")
+    level(T.data0[:, 128 * me + 1:128 * me + 128], c("keepo"), on="sb")
+    act(new("init2"), T.ee[:, PLACE:PLACE + 1], scale=-float(LAND + M), bias=c("u2"), free=True, on="sb")
+    for r in range(N):
+        kw2 = act(T.bs[:, r:r + 1], e2(N0), scale=float(CAP * others.index(r) - LAND) if r != me else -1.0, bias=T.bt0[:, r:r + 1], free=True, on="sb")
+    kc0 = act(T.c0m[:], T.vs1[:], scale=e2(N0), bias=T.bs[:, me:me + 1], on="*", after=[kvs1, kw2])
 
-    tt(T.val3[:], T.s3[:].indirect(T.offsel[:, 0:16]), T.vsel[:], A.add, free=True)
-    wait(v, "v", "g4", 2)
-    cp(T.w3[:].indirect(T.off3[:, 0:16]), T.val3[:], after=[("sz", cnt["sz"])])
-    cp(T.dp[:, 0:24:2, :], T.w3[:, 256:448])
-    cp(T.dp[:, 1:24:2, :], T.w3[:, 256:448], free=True)
-    vec(v.transpose, T.t3[:], T.w3[:, 256:448], free=True, on="su")
-    vec(v.transpose, T.tp[:], T.dp[:])
-    tt(T.c3[:, :, 13:15], T.t3[:, :, 13:15], T.t3[:, :, 29:31], A.add, on="su")
-    kyy = tt(T.yy[:], T.tp[:, :, 0:10], T.tp[:, :, 16:26], A.add)
-    kpl = vec(v.transpose, T.pl[:], T.c3[:], on="su")
-    cp(T.qbc[0:32, 0:12], T.yy[0:32, :, 3], free=True, on="so", after=[kyy])
-    cp(T.qbc[0:32, 12:24], T.yy[0:32, :, 9], free=True, on="so")
-    tt(T.x3[:, :, 0:3], T.yy[:, :, 0:3], T.kc[:], A.add, after=[kkc])
-    ts(T.x3[:, :, 3], T.yy[:, :, 8], float(LAND), A.add, free=True)
-    cp(T.qbc[32:64, :], T.qbc[0:32, :], on="so")
-    tt(T.x3m[:], T.x3[:], T.yy[:, :, 4:8], A.mult)
-    kqbc = cp(T.qbc[64:128, :], T.qbc[0:64, :], on="so")
-    ky4 = scan(T.y4[:], T.rs[:, 0:48], T.x3m[:], 0.0)
-    for b in range(0, 128, 32):
-        kq0 = cp(T.q0[b:b + 32, :], T.y4[0:32, 3:48:4], free=True, on="so", after=[ky4])
+    fill(T.rs[:, 0:48:4], 0.0, free=False, on="sz")
+    fill(T.w1[:, 128:272], 0.0, on="sz")
+    cp(T.gg1[:], T.winb[:, 0:4].indirect(rk), after=[kw1])
+    cp(T.offsel[:], T.io32[:], free=True, on="sf")
+    cp(T.off2[:], T.io32[:], free=True, on="sf")
+    kso = fill(T.s2[:, 512:640], 0.0, on="sf")
+    scan(T.gs1[B0], T.d01[B0], T.gg1[B0], c("init1")[B0])
+    fill(T.rs7[:], 1.0, on="se")
+    turn(T.tg[B0], T.gs1[B0])
+    fill(T.rs7[:, 0:112:7], 0.0, free=False, on="se")
+    tt(T.x1[B0], T.tg[B0, :, 0:4], T.tg[B0, :, 16:20], A.mult)
+    kxq = vec(v.quantize_mx, T.xq[:], T.xs[:], T.xb[:], free=True, on="*", after=[("dx", 16)])
+    scan(T.y1[B0], T.rs[B0, 0:16], T.x1[B0], 0.0, after=[last("sz")])
+    ts(T.off1[B0], T.y1[B0, 3:16:4], 128.0, A.add)
+    iota(T.w2[:, 0:M + LAND], [[0, M + LAND]], "g4")
+    cp(T.w1[:].indirect(T.off1[:]), T.vs1[:], after=[kvs1])
+    cp(T.d1[B0, 0:18:2, :], T.w1[B0, 128:272])
+    cp(T.d1[B0, 1:18:2, :], T.w1[B0, 128:272], free=True)
+    turn(T.td1[B0], T.d1[B0])
+    for b in range(2):
+        tt(T.l1f[32 * b:32 * b + 32], T.td1[B0, :, 0], T.td1[B0, :, 16], A.add, free=b > 0)
+    for b in range(2):
+        kl = ts(T.list1[64 * b:64 * b + 64, 0:9], T.l1f[0:64], -1.0, A.add, free=b > 0)
+    kpk = cp(words(T.pk1[:]), words(T.xq[:]).indirect(T.list1[:, 0:9]), after=[kxq])
+    ksc = act(T.ps1[:], T.xs[:].indirect(T.list1[:, 0:9]), C.Copy, on="*", after=[kl, kxq])
+    to_rest([kpk], 0, s.f1c, lambda k: raw(T.pk1[:, CAP * k:CAP * k + CAP]), raw(T.fc1[:]))
+    to_rest([ksc], 1, s.f1s, lambda k: T.ps1[:, CAP * k:CAP * k + CAP], T.fs1[:])
+    to_peer([kpk], s.c1, lambda k: raw(T.pk1[:, CAP * k:CAP * k + CAP]), raw(T.cb[:, CAP * at:CAP * at + CAP]))
+    to_peer([ksc], s.c1, lambda k: T.ps1[:, CAP * k:CAP * k + CAP], T.cbs[:, CAP * at:CAP * at + CAP])
+
+    here = slice(512 * me, 512 * me + 512)
+    dma(g.sync, T.win[GOES:GOES + 4, here], T.mk[:], "drow", after=[km, kwme])
+    dma(g.sync, T.win[SENT:SENT + 3, here], T.mk[0:96], "drow")
+    dma(g.sync, T.win[PLACE:PLACE + 4, here], T.gt[:, 16 * me:16 * me + 16], "drow")
+    dma(g.sync, T.wb[:], T.w[:], "dw")
+    for k in (peer, 0, 1):
+        there = slice(512 * others[k], 512 * others[k] + 512)
+        dma(g.sync, T.win[PLACE:PLACE + 4, there], T.gl[k], "drow", after=[kreg[k], ("m0%d" % k, 8)])
+        dma(g.sync, T.win[SLOT + k:SLOT + k + TWIN + 1:TWIN, there], T.gl[k, 0:64], "drow")
+    dma(g.sync, raw(T.cb[:, LAND:LAND + TX]), raw(T.xq[:]), "dcb", after=[kxq])
+    dma(g.sync, T.cbs[:, LAND:LAND + TX], T.xs[:], "dcb")
+    dma(g.sync, raw(T.lp[:, 96:176]), raw(T.xq[:, 0:80]), "dcb")
+    dma(g.sync, T.lps[:, 96:176], T.xs[:, 0:80], "dcb")
+
+    ready = [("m1", 24), last("drow"), ku]
+    kgb = act(T.g2[:, 256:512], T.win[:].indirect(T.ul[:, 16:32]), C.Copy, on="sa", after=ready)
+    cp(T.g2[:, 0:256], T.win[:].indirect(T.ul[:, 0:16]), on="sx", after=ready)
+    ks = scan(T.s2[:, 0:512], T.data0[:], T.g2[:], c("init2"), on="sx", after=[kgb, kw2])
+    for n, r in enumerate(others):
+        kvsel = act(T.vsel[:, 64 * r:64 * r + 64], T.s2[:].indirect(T.offsel[:, 4 * r:4 * r + 4]), bias=T.bs[:, r:r + 1], free=n > 0, on="sa", after=[ks, kso])
+    turn(T.tg2[B0], T.s2[B0, 0:512], on="sx")
+    tt(T.vsel[:, 64 * me:64 * me + 64], T.s2[:].indirect(T.offsel[:, 4 * me:4 * me + 4]), T.c0m[:], A.add, free=True, on="so", after=[kso, kc0])
+    for k in range(3):
+        tt(T.x2[B0, k:112:7], T.tg2[B0, :, SENT + k], T.tg2[B0, :, GOES + k], A.mult, free=k > 0, on="sx")
+    tt(T.x2[B0, 3:112:7], T.tg2[B0, :, PLACE], T.tg2[B0, :, ENDS], A.mult, free=True, on="sx")
+    tt(T.x2[B0, 4:112:7], T.tg2[B0, :, ENDS], T.ntr[B0], A.mult, free=True, on="sx", after=[("g3", 2)])
+    tt(T.x2[B0, 5:112:7], T.tg2[B0, :, LEAVES], T.ntr[B0], A.mult, free=True, on="sx")
+    scan(T.y2[B0], T.rs7[B0], T.x2[B0], 0.0, on="sx", after=[last("se")])
+    kq2 = quant(2)
+    ts(T.off2[B0], T.y2[B0, 6:112:7], float(M), A.add, on="sx")
+    kq1 = quant(1)
+    kw = cp(T.w2[:].indirect(T.off2[:]), T.vsel[:], on="sx", after=[last("so"), kvsel, ("g4", 1)])
+    kwq = quant(0)
+    wait(v, "v", *kw)
 
     def w(k):
         return T.wq[:, 128 * k:128 * k + 128], T.ws[:, 128 * k:128 * k + 128]
-    m2 = mm(T.ps[:, 1024:1280], *w(2), T.xq[:], T.xs[:], True, True, free=True, after=[kwq])
-    m1 = mm(T.ps[:, 512:768], *w(1), T.xq[:], T.xs[:], True, True)
-    wait(g.tensor, "t", "c1", 48)
-    wait(g.tensor, "t", "dcb", 64)
-    m0 = mm(T.ps[:, 0:400], *w(0), T.cb[:], T.cbs[:], True, True)
-    act(T.cw[:, 1:257], T.ps[:, 1024:1280], C.Copy, on="sb", after=[m2])
-    act(T.bw[:, 1:257], T.ps[:, 512:768], C.Copy, free=True, on="sb", after=[m1])
-    kaw = act(T.aw[:, 1:401], T.ps[:, 0:400], C.Copy, free=True, on="sb", after=[m0])
-    wait(a, "a", *kaw)
-    kt1 = act(T.t1[:], T.cw[:, 0:257].indirect(T.qbc[:, 0:12]), C.Copy, on="sa", after=[kqbc])
-    kid = act(T.idl[:], T.pl[:], bias=-1.0, on="sa", after=[kpl])
-    wait(g.sync, "s", *kid)
-    g.sync.dma_start(T.id[0:1, :], T.idl[13:14, :]).then_inc(s.did, 16)
-    g.sync.dma_start(T.id[1:2, :], T.idl[14:15, :]).then_inc(s.did, 16)
-    tt(T.t2[:], T.bw[:, 0:257].indirect(T.qbc[:, 12:24]), T.t1[:], A.add, on="so", after=[kaw, kqbc, kt1])
+    m2 = mm(T.ps[:, 1024:1280], *w(2), T.xq[:], T.xs[:], True, True, free=True, after=[kq2, kxq])
+    m1 = mm(T.ps[:, 512:768], *w(1), T.xq[:], T.xs[:], True, True, after=[kq1])
+    m0 = mm(T.ps[:, 0:400], *w(0), T.cb[:], T.cbs[:], True, True, after=[kwq, ("c1", 48), last("dcb")])
+    for x, at0 in ((T.aw, LAND), (T.bw, 0), (T.cw, 0)):
+        level(x[:, at0:at0 + 1], 0.0, free=True, on="sb")
+    act(new("idb"), c("even"), C.Copy, scale=-1.0, free=True, on="sb")
+    act(T.cw[:, 1:257], T.ps[:, 1024:1280], C.Copy, free=True, on="sb", after=[m2])
+    kbw = act(T.bw[:, 1:257], T.ps[:, 512:768], C.Copy, free=True, on="sb", after=[m1])
+    kid = act(T.idl[:], T.w2[:, 0:M], bias=c("idb"), on="sk", after=[kw, kbw])
+    dma(g.sync, T.id[:], T.idl[ID0:ID0 + 2, :], "did", after=[kid])
 
-    wait(g.tensor, "t", "c2p", 16)
-    mm(T.ps[:, 2048:2176], *w(0), T.lp[:, 0:128], T.lps[:, 0:128], True, False)
+    cp(T.d2[B0, 0:18:2, :], T.w2[B0, M:M + LAND], after=[kpk])
+    cp(T.d2[B0, 1:18:2, :], T.w2[B0, M:M + LAND], free=True)
+    cp(T.dp[B0, 0:24:2, :], T.w2[B0, 0:M], free=True, on="sd")
+    turn(T.td2[B0], T.d2[B0])
+    cp(T.dp[B0, 1:24:2, :], T.w2[B0, 0:M], free=True, on="sd")
+    for b in range(2):
+        for h, r in enumerate((N0, C1)):
+            tt(T.nf[32 * b:32 * b + 32, :, h, :], T.td2[B0, :, :, r], T.td2[B0, :, :, TWIN + r], A.add, free=b + h > 0)
+    turn(T.tp[B0], T.dp[B0], on="sd")
+    for b in range(2):
+        kl2 = ts(T.list2[64 * b:64 * b + 64], T.nf[0:64], LAND - 1.0, A.add, free=b > 0)
+    tt(T.qz[B0, 0:12], T.tp[B0, :, C1], T.tp[B0, :, TWIN + C1], A.add, on="sd")
+    tt(T.qz[B0, 12:24], T.tp[B0, :, C2], T.tp[B0, :, C2 + 1], A.add, free=True, on="sd")
+    landed = [("c1", 48), last("dcb")]
+    ksa = act(T.ps2[:, 0:192], T.cbs[:].indirect(T.list2[:, 0:12]), C.Copy, on="sa", after=[kl2] + landed)
+    ksb = act(T.ps2[:, 192:288], T.cbs[:].indirect(T.list2[:, 12:18]), C.Copy, on="*")
+    kpa = cp(words(T.pk2[:, 0:192]), words(T.cb[:]).indirect(T.list2[:, 0:12]), after=landed)
+    kpb = cp(words(T.pk2[:, 192:288]), words(T.cb[:]).indirect(T.list2[:, 12:18]), free=True, on="so")
+    to_rest([kpa], 0, s.f2c, lambda k: raw(T.pk2[:, 96 * k:96 * k + 96]), raw(T.fc2[:]))
+    to_rest([ksa], 1, s.f2s, lambda k: T.ps2[:, 96 * k:96 * k + 96], T.fs2[:])
+    to_peer([kpb], s.c2p, lambda k: raw(T.pk2[:, 96 * k:96 * k + 96]), raw(T.lp[:, 0:96]))
+    to_peer([ksb], s.c2p, lambda k: T.ps2[:, 96 * k:96 * k + 96], T.lps[:, 0:96])
+    g.wait_ge(s.did, 16)
+    g.dma_start(T.id[:], T.idl[TWIN + ID0:TWIN + ID0 + 2, :], accum_op=A.add).then_inc(s.dia, 16)
+
+    tt(T.z3[B0], T.tp[B0, :, N0], T.tp[B0, :, TWIN + N0], A.add, free=True, on="sd")
+    tt(T.fl[B0, :, 0:3], T.tp[B0, :, ON:ON + 3], T.tp[B0, :, TWIN + ON:TWIN + ON + 3], A.add, free=True, on="sd")
+    tt(T.x3[B0, :, 0:3], T.tp[B0, :, SLOT:SLOT + 3], T.tp[B0, :, TWIN + SLOT:TWIN + SLOT + 3], A.add, free=True, on="sd")
+    ts(T.fl[B0, :, 3], T.qz[B0, 0:12], 1.0, A.min, on="sd")
+    ts(T.x3[B0, :, 3], T.z3[B0], float(LAND), A.add, free=True, on="sd")
+    for b in range(0, 128, 32):
+        kqbc = cp(T.qbc[b:b + 32], T.qz[B0], free=True, on="sc")
+    tt(T.x3m[B0], T.x3[B0], T.fl[B0], A.mult, on="sd")
+    kaw = act(T.aw[:, LAND + 1:LAND + 401], T.ps[:, 0:400], C.Copy, free=True, on="sb", after=[m0])
+    kt1 = act(T.t1[:], T.cw[:, 0:257].indirect(T.qbc[:, 12:24]), C.Copy, on="sa", after=[kqbc, kbw])
+    scan(T.y4[B0], T.rs[B0], T.x3m[B0], 0.0, on="sd")
+    for b in range(0, 128, 32):
+        kq0 = ts(T.q0[b:b + 32], T.y4[B0, 3:48:4], float(LAND), A.add, free=b > 0, on="sd")
+    tt(T.t2[:], T.bw[:, 0:257].indirect(T.qbc[:, 0:12]), T.t1[:], A.add, on="so", after=[kqbc, kt1])
+
+    mm(T.ps[:, 2048:2176], *w(0), T.lp[:, 0:128], T.lps[:, 0:128], True, False, after=[("c2p", 16)])
     mp = mm(T.ps[:, 2048:2176], *w(1), T.lp[:, 48:176], T.lps[:, 48:176], False, True, free=True)
-    wait(g.tensor, "t", "c2", 32)
-    mm(T.ps[:, 1536:1680], *w(0), T.lr[:, 0:144], T.lrs[:, 0:144], True, False)
+    mm(T.ps[:, 1536:1680], *w(0), T.lr[:, 0:144], T.lrs[:, 0:144], True, False, after=[("c2", 32)])
     mr = mm(T.ps[:, 1536:1680], *w(1), T.lr[:, 48:192], T.lrs[:, 48:192], False, True, free=True)
-    kpw = act(T.aw[:, 545:593], T.ps[:, 2048:2096], C.Copy, free=True, on="sb", after=[mp])
-    cp(T.aw[:, 401:545], T.ps[:, 1536:1680], free=True, on="so", after=[mr])
-    ky = tt(T.yo[:], T.aw[:, 0:593].indirect(T.q0[:, 0:12]), T.t2[:], A.add, on="so", after=[kq0, kpw])
-    wait(g.sync, "s", *ky)
-    g.sync.dma_start(T.y[:], T.yo[:]).then_inc(s.dy, 16)
+    kpw = act(T.aw[:, 96:144], T.ps[:, 2048:2096], C.Copy, free=True, on="sb", after=[mp])
+    for k in rest:
+        cp(T.aw[:, CAP * k:CAP * k + CAP], T.ps[:, 1536 + 96 * k:1536 + 96 * k + CAP], free=True, on="so", after=[mr])
+    ky = tt(T.yo[:], T.aw[:, 0:LAND + 401].indirect(T.q0[:]), T.t2[:], A.add, on="so", after=[kq0, kpw])
+    dma(g.sync, T.y[:], T.yo[:], "dy", after=[ky])
 
-    g.wait_ge(s.dy, 16)
-    g.wait_ge(s.did, 32)
-    for x in ("sv", "su", "so", "sz", "sq", "sa", "sb", "sk", "sp", "st", "loc"):
-        wait(g, "g", x, cnt[x])
+    g.wait_ge(s.dia, 16)
+    for x in CHAINS + ["loc", "dy"]:
+        if max([n for (q, y), n in known.items() if y == x] + [0]) < cnt.get(x, 0):
+            wait(g, "g", x, cnt[x])

@@ -5,8 +5,9 @@ N, CAP, TX, M = 4, 48, 256, 192
 LAND = 3 * CAP
 F, B, I, U = "float32", "bfloat16", "int32", "uint16"
 CODE, PLANE = "float8_e4m3fn_x4", "uint8"
-ON, C1, ID0, ID1, N0, SLOT, SENT, PLACE, ENDS, C2, GOES, LEAVES = 0, 3, 4, 5, 6, 7, 10, 13, 14, 15, 17, 20
+ON, SLOT, C1, ID0, ID1, N0, SENT, PLACE, ENDS, C2, GOES, LEAVES = 0, 3, 6, 7, 8, 9, 10, 13, 14, 15, 17, 20
 PAIRED, TWIN = 10, 22
+FEW = 2
 
 
 def _sb(d, *s):
@@ -18,16 +19,19 @@ SCRATCH = {
     "xq": _sb(CODE, 256), "xs": _sb(PLANE, 256), "cb": _sb(CODE, 400), "cbs": _sb(PLANE, 400), "wq": _sb(CODE, 384), "ws": _sb(PLANE, 384),
     "pk1": _sb(CODE, 144), "ps1": _sb(PLANE, 144), "pk2": _sb(CODE, 288), "ps2": _sb(PLANE, 288),
     "fc1": _sb(CODE, 48), "fs1": _sb(PLANE, 48), "fc2": _sb(CODE, 96), "fs2": _sb(PLANE, 96),
-    "fu": _sb(U, 8), "fn": ("dram", [128, 16], B), "gt": _sb(B, 64), "gl": ("dram", [3, 128, 16], B),
-    "lr": _sb(CODE, 192), "lrs": _sb(PLANE, 192), "lp": _sb(CODE, 176), "lps": _sb(PLANE, 176),
+    "fu": _sb(F, 8), "fn": ("dram", [128, 16], B), "gt": _sb(B, 64), "gl": ("dram", [3, 128, 16], B),
+    "lr": _sb(CODE, 192), "lrs": _sb(PLANE, 192), "lp": _sb(CODE, 224), "lps": _sb(PLANE, 224),
     "pmi": _sb(F, 32), "ee": _sb(F, 32), "e2": _sb(F, 10), "e16": _sb(F, 4), "col": _sb(F, 32), "io32": _sb(I, 16), "io4": _sb(F, 4),
     "io256": _sb(B, 256), "d01": _sb(B, 128), "offsel": _sb(U, 16), "ntr": _sb(F, 16), "data0": _sb(B, 512),
-    "rs": _sb(F, 48), "rs7": _sb(F, 112), "half": _sb(B, 16), "winb": _sb(B, 16), "bs": _sb(F, 4), "bt0": _sb(F, 4),
-    "stb": _sb(I, 16), "b0": _sb(I, 8), "sx": _sb(I, 8), "sy": _sb(I, 8), "sz": _sb(I, 8), "sw": _sb(I, 8),
-    "lists": _sb(U, 48), "p1w": _sb(I, 512), "b1r": _sb(B, 256), "nd": _sb(F, 256), "tn": _sb(F, 8, 32), "ul": _sb(U, 32),
+    "rs": _sb(F, 48), "rs7": _sb(F, 112), "btl": ("dram", [128, 2], I), "fb": ("dram", [128, 2], I), "bl": ("dram", [3, 128, 2], I),
+    "btr": _sb(I, 32), "ulf": _sb(F, 32), "ux": _sb(F, 32),
+    "data3": _sb(B, 192), "w3": _sb(B, 192), "on3": _sb(F, 3), "v3": _sb(F, 3),
+    "winb": _sb(B, 16), "bs": _sb(F, 4), "bt0": _sb(F, 4),
+    "stb": _sb(I, 8), "b0": _sb(I, 4), "sx": _sb(I, 4), "sy": _sb(I, 4), "sz": _sb(I, 4), "sw": _sb(I, 4),
+    "lists": _sb(U, 64), "p1w": _sb(I, 512), "nd": _sb(F, 128), "tn": _sb(F, 4, 32), "ul": _sb(U, 32),
     "nxs": _sb(I, 32), "nxt": _sb(I, 32), "nxr": _sb(I, 16), "mk": _sb(B, 16), "win": _sb(B, 2048),
-    "gg1": _sb(B, 128), "gs1": _sb(B, 128), "tg": _sb(B, 4, 32), "x1": _sb(F, 16), "y1": _sb(F, 16), "off1": _sb(U, 4),
-    "vs1": _sb(B, 64), "c0m": _sb(B, 64), "w1": _sb(B, 272), "d1": _sb(B, 18, 16), "td1": _sb(B, 9, 32), "l1f": _sb(F, 9), "list1": _sb(U, 10),
+    "gg1": _sb(B, 128), "gs1": _sb(B, 128), "sg": _sb(B, 384), "acc": _sb(F, 3), "slot3": _sb(F, 3), "p15": _sb(I, 1), "sth": _sb(I, 16),
+    "vs1": _sb(B, 64), "c0m": _sb(B, 64), "list1": _sb(U, 10), "pk0": _sb(CODE, 144), "ps0": _sb(PLANE, 144),
     "g2": _sb(B, 512), "s2": _sb(B, 640), "tg2": _sb(B, 16, 32), "x2": _sb(F, 112), "y2": _sb(F, 112), "off2": _sb(U, 16),
     "vsel": _sb(B, 256), "w2": _sb(B, 848), "d2": _sb(B, 18, 16), "td2": _sb(B, 3, 3, 32), "nf": _sb(F, 3, 2, 3), "list2": _sb(U, 18),
     "idl": _sb(F, 192), "dp": _sb(B, 24, 16), "tp": _sb(B, 12, 32), "fl": _sb(F, 12, 4), "x3": _sb(F, 12, 4), "z3": _sb(F, 12), "qz": _sb(F, 24),
@@ -35,9 +39,9 @@ SCRATCH = {
     "ps": ("psum", [128, 2560], F), "aw": _sb(F, 552), "bw": _sb(F, 264), "cw": _sb(F, 264),
     "t1": _sb(F, 192), "t2": _sb(F, 192), "yo": _sb(F, 192),
 }
-SINGLE = ["k%d" % n for n in range(24)]
-CHAINS = ["sv", "su", "so", "sz", "sq", "sc", "sd", "se", "sf", "sa", "sb", "sk", "sp", "st", "sx", "t0", "t1", "t2", "r0", "r1", "r2", "r3"] + SINGLE
-SEMAPHORES = CHAINS + ["g0", "g1", "g2", "g3", "g4", "g5", "dst", "dbt", "ds1", "dnx", "dns", "dx", "dw", "dcb", "drow", "dy", "did", "dia",
+SINGLE = ["k%d" % n for n in range(32)]
+CHAINS = ["sv", "su", "so", "sz", "sq", "sc", "sd", "se", "sf", "sa", "sb", "sk", "sp", "st", "sx", "s3", "s4", "s5", "s6", "s7", "s8", "t0", "t1", "t2", "r0", "r1", "r2", "r3"] + SINGLE
+SEMAPHORES = CHAINS + ["g0", "g1", "g2", "g3", "g4", "dbl", "dbo", "fb", "mb0", "mb1", "mb2", "dst", "dbt", "ds1", "dnx", "dns", "dx", "dw0", "dw1", "dw2", "drow", "dy", "did", "dia",
                        "m00", "m01", "m02", "m1", "c1", "c2", "c2p", "loc", "f0", "f1", "f1c", "f1s", "f2c", "f2s"]
 
 
@@ -64,18 +68,20 @@ def hand_on(g, core, T, topo):
             rid, pid = topo.addr(dst, core)
             e = topo.engines(core, dst)
             s = T.sem
+            half = len(topo.engines(src, core)) // 2
             if h:
-                jobs = [(s.f1s, T.cbs[:, CAP * k:CAP * k + CAP], T.fs1[:], s.c1),
-                        (s.f2s, T.lrs[:, 96 * k:96 * k + 96], T.fs2[:], s.c2)]
-            else:
-                jobs = [(s.f0, T.gl[k], T.fn[:], s["m0%d" % k]),
-                        (s.f1, T.ul[:, 8 * i:8 * i + 8], T.fu[:], s.m1),
-                        (s.f1c, T.cb[:, CAP * k:CAP * k + CAP].bitcast(dt.uint8), T.fc1[:].bitcast(dt.uint8), s.c1),
-                        (s.f2c, T.lr[:, 96 * k:96 * k + 96].bitcast(dt.uint8), T.fc2[:].bitcast(dt.uint8), s.c2)]
-            for sem, out, in_, to in jobs:
-                g.wait_ge(sem, len(topo.engines(src, core)) // 2)
-                g.remote_dma(out, in_, to, s.loc, pid, rid, mask_of(e))
-            g.wait_ge(s.loc, len(jobs) * len(e))
+                continue
+            jobs = [(s.fb, 1, e, T.bl[k], T.fb[:], s["mb%d" % k]),
+                    (s.f0, half // 2, e[:FEW], T.gl[k], T.fn[:], s["m0%d" % k]),
+                    (s.f1, half, e, T.ulf[:, 8 * i:8 * i + 8], T.fu[:], s.m1),
+                    (s.f1s, half, e, T.cbs[:, CAP * k:CAP * k + CAP], T.fs1[:], s.c1),
+                    (s.f1c, half, e, T.cb[:, CAP * k:CAP * k + CAP].bitcast(dt.uint8), T.fc1[:].bitcast(dt.uint8), s.c1),
+                    (s.f2c, half, e, T.lr[:, 96 * k:96 * k + 96].bitcast(dt.uint8), T.fc2[:].bitcast(dt.uint8), s.c2),
+                    (s.f2s, half, e, T.lrs[:, 96 * k:96 * k + 96], T.fs2[:], s.c2)]
+            for sem, n, use, out, in_, to in jobs:
+                g.wait_ge(sem, n)
+                g.remote_dma(out, in_, to, s.loc, pid, rid, mask_of(use))
+            g.wait_ge(s.loc, sum(len(job[2]) for job in jobs))
 
 
 def rank_program(g, core, T, topo):
@@ -139,7 +145,7 @@ def rank_program(g, core, T, topo):
 
     def quant(k):
         return vec(v.quantize_mx, T.wq[:, 128 * k:128 * k + 128], T.ws[:, 128 * k:128 * k + 128], T.wb[:, 512 * k:512 * k + 512], free=True, on="*",
-                   after=[("dw", 16)])
+                   after=[("dw%d" % k, 16)])
 
     def dma(q, out, in_, sem, after=()):
         for x in after:
@@ -193,20 +199,28 @@ def rank_program(g, core, T, topo):
         return T.e2[:, r:r + 1]
 
     G0, B0 = slice(0, 16), slice(0, 32)
-    q1l, btu, qsel, rk = T.lists[:, 0:16], T.lists[:, 16:32], T.lists[:, 32:36], T.lists[:, 40:48]
-    mine = T.ul[:, 8 * me:8 * me + 8]
+    q1l, qsel, rk, stu = T.lists[:, 0:8], T.lists[:, 32:36], T.lists[:, 40:48], T.lists[:, 48:57]
+    mine = T.ulf[:, 8 * me:8 * me + 8]
 
+    for h, q in enumerate((g.sync, a)):
+        dma(q, T.btl[64 * h:64 * h + 64, :], T.bt[:], "dbl")
+    for h in range(2):
+        dma(g.sync, T.sth[16 * h:16 * h + 16, 0:8 - h], T.st[:, h:8], "dst")
+        dma(a, T.sth[16 * h:16 * h + 16, 8:16 - h], T.bt[:, h:8], "dbt")
     for b in range(0, 128, 32):
         dma(g.sync if b < 64 else a, T.nxs[b + 16:b + 32, :], T.nx[:], "dns")
-    dma(g.sync, T.stb[0:16, 0:8], T.st[:], "dst")
-    dma(a, T.stb[0:16, 8:16], T.bt[:], "dbt")
-    dma(a, T.stb[16:32, 0:7], T.st[:, 1:8], "ds1")
+    for h in range(2):
+        dma(a, T.stb[16 * h:16 * h + 16, :], T.st[:], "ds1")
     kp = fill(T.p1w[:], 0, on="*")
-    dma(g.sync, T.p1w[0:1, :], T.nx[:], "dnx", after=[kp])
+    for h, q in enumerate((g.sync, a)):
+        dma(q, T.p1w[16 * h:16 * h + 1, :], T.nx[:], "dnx", after=[kp])
     dma(g.sync, T.xb[:], T.x[:], "dx")
+    dma(g.sync, T.wb[:, 1024:1536], T.w[:, 1024:1536], "dw2")
     iota(T.pmi[:], [[-1, 32]], "g0", by=1)
-    iota(T.half[:, 0:4], [[1, 2], [0, 2]], "g5")
+    dma(g.sync, T.btr[B0, 8 * me:8 * me + 8], T.btl[:], "dbo", after=[last("dbl")])
     iota(T.io256[:], [[1, 256]], "g2", base=1)
+    call([last("dbl")], [(forwarders(topo, core, T.cores[others[k]])[0], 14 + k, 16, s.fb, T.btl[:], T.fb[:]) for k in rest]
+         + [(T.cores[others[peer]], 0, 8, s["mb%d" % at], T.btl[:], T.bl[at])])
     g.iota(T.io32[:], [[32, 16]], 0, 1).then_inc(s.g1, 1)
     iota(T.io4[:], [[1, 4]], "g1", base=1)
     iota(T.ntr[:], [[-32, 16]], "g3", base=-LAND, by=-1)
@@ -215,12 +229,10 @@ def rank_program(g, core, T, topo):
     p = T.pmi[:, 0:1]
     ts(T.ee[:], T.pmi[:], 0.0, A.is_equal, on="sc", after=[("g0", 1)])
     ts(new("m22"), p, float(TWIN), A.is_ge, -float(TWIN), A.mult, free=True, on="sc")
-    ts(new("even"), p, 16.0, A.is_lt, free=True, on="sc")
     for b in range(0, 128, 32):
         fill(T.nxs[b:b + 16, :], 0, on="su")
     klists = fill(T.lists[:], 0, on="*")
     tt(T.e2[:], T.ee[:, 0:PAIRED], T.ee[:, TWIN:TWIN + PAIRED], A.add, on="sc")
-    tt(T.e16[:], T.ee[:, 0:4], T.ee[:, 16:20], A.add, free=True, on="sc")
     ke = tt(new("pp"), p, c("m22"), A.add, free=True, on="sc")
 
     def column(e, on):
@@ -228,125 +240,128 @@ def rank_program(g, core, T, topo):
 
     def ends(e, on):
         return ts(T.gt[0:64, 16 * e:16 * e + 16], T.nxr[0:64], float(e), A.is_equal, free=True, on=on, after=[kr])
+    ts(T.sx[B0], T.sth[B0, 0:8:2], 513.0, A.mult, free=True, on="sx", after=[("dst", 32)])
+    ts(T.b0[B0], T.sth[B0, 8:16:2], 32.0, A.mult, free=True, on="sx", after=[("dbt", 32)])
+    kon = tt(T.on3[:], T.e2[:, ON:ON + 3], T.e2[:, SLOT:SLOT + 3], A.add, free=True, on="*", after=[ke])
     turn(T.nxt[:], T.nxs[:], on="su", after=[("dns", 64)])
-    ts(T.sx[G0], T.stb[G0, 0:8], 513.0, A.mult, free=True, on="sx", after=[("dst", 16)])
-    ts(T.b0[G0], T.stb[G0, 8:16], 32.0, A.mult, free=True, on="sx", after=[("dbt", 16)])
-    cp(btu[G0, 0:16:2], T.stb[G0, 8:16], free=True, on="sp", after=[klists])
+    ts(T.sw[B0], T.sx[B0], 3, A.logical_shift_right, 511, A.bitwise_and, on="sx")
+    ts(T.sy[B0], T.b0[B0], 32, A.bitwise_and, free=True, on="sx")
     kr = ts(T.nxr[:], T.nxt[:, 16:32], 8, A.logical_shift_right, on="su")
-    kb = cp(btu[G0, 1:16:2], T.stb[G0, 8:16], free=True, on="sp")
-    for k in rest:
-        column(others[k], "t0")
+    column(others[0], "t0")
+    tt(T.sz[B0], T.sw[B0], T.sy[B0], A.add, on="sx")
+    column(others[1], "t0")
     for k in rest:
         ends(others[k], "t0")
-    ts(T.sw[G0], T.sx[G0], 3, A.logical_shift_right, 511, A.bitwise_and, on="sx")
-    ts(T.sy[G0], T.b0[G0], 32, A.bitwise_and, free=True, on="sx")
+    cp(q1l[B0, 0:8:2], T.sz[B0], on="sx", after=[klists])
+    cp(q1l[B0, 1:8:2], T.sz[B0], free=True, on="sx")
     ends(others[peer], "t1")
     column(others[peer], "t1")
-    ts(new("le13"), c("pp"), PLACE + 0.5, A.is_lt, free=True, on="sd", after=[ke])
-    tt(T.sz[G0], T.sw[G0], T.sy[G0], A.add, on="sx")
-    kq = cp(qsel[B0], T.stb[B0, 0:8:2], free=True, on="*", after=[("ds1", 16)])
-    ts(new("keep"), c("pp"), float(ID1), A.is_ge, c("le13"), A.mult, on="sd")
-    kk = ts(new("keepr"), c("pp"), float(SLOT), A.is_ge, c("le13"), A.mult, free=True, on="sd")
-    cp(q1l[G0, 0:16:2], T.sz[G0], on="sx")
-    cp(q1l[G0, 1:16:2], T.sz[G0], free=True, on="sx")
-    kmine = fill(mine, 0, on="*")
     wait(a, "a", *ke)
-    for r in range(N):
-        k = others.index(r) if r != me else 3
-        act(T.winb[:, r:r + 1], T.e16[:, k:k + 1], C.Copy, free=True)
-    kh = act(T.b1r[:], T.half[:, 0:4].indirect(btu), C.Copy, scale=0.5, free=True, on="*", after=[kb, ("g5", 1)])
-    act(new("u1"), p, scale=48.0, bias=-1.0, free=True)
-    act(new("vme"), e2(ID1), bias=e2(N0), free=True)
-    for k in range(3):
-        act(new("v%d" % k), e2(ON + k), bias=e2(ID1), free=True)
-    ends(me, "t2")
-    column(me, "t2")
-    tt(T.nd[:], T.p1w[:].indirect(q1l), T.b1r[:], A.add, on="sx", after=[("dnx", 16), kh])
-    to_rest([last("t0")], 0, s.f0, lambda k: T.gt[:, 16 * others[k]:16 * others[k] + 16], T.fn[:])
+    wait(a, "a", "g2", 1)
+    kvme = act(new("vme"), e2(ID1), bias=e2(N0), free=True, on="*")
+    goal = new("goal")
+    for k, r in enumerate(others + [me]):
+        kgoal = act(goal[32 * k:32 * k + 32], T.io256[32 * k:32 * k + 32, 0:1], scale=0.0, bias=r + 1.0, free=True, on="s8")
+    kone = level(T.d01[:], 1.0, free=True, on="*")
+    act(new("u2"), c("pp"), scale=float(CAP), bias=-1.0 - CAP * SENT, free=True, on="sb")
+    act(T.bt0[:], T.io4[:], C.Copy, scale=e2(ID0), free=True, on="sb", after=[("g1", 2)])
+    for h in range(2):
+        kwme = act(T.win[:, 512 * me + h:512 * me + 512:2], T.io256[:], scale=e2(C1), bias=c("vme"), free=True, on="r3", after=[kvme])
+    ts(T.nd[:], T.p1w[:].indirect(q1l), 4.0, A.mult, on="sx", after=[("dnx", 32)])
+    call([last("t0")], [(forwarders(topo, core, T.cores[others[k]])[0], 2 + k, 4, s.f0, T.gt[:, 16 * others[k]:16 * others[k] + 16], T.fn[:]) for k in rest])
     to_peer([last("t1")], s["m0%d" % at], lambda k: T.gt[:, 16 * others[k]:16 * others[k] + 16], T.gl[at])
-    for k in range(3):
-        ts(T.mk[32 * k:32 * k + 32], T.nxr[32 * k:32 * k + 32], float(others[k]), A.is_equal, free=True, on="t2")
+    kmine = fill(mine, 0.0, on="*")
+    ts(T.p15[:], T.io32[:, 0:1], 15, A.bitwise_and, on="sc", after=[("g1", 2)])
+    ts(new("le13"), c("pp"), PLACE + 0.5, A.is_lt, free=True, on="sd")
     ktn = turn(T.tn[B0], T.nd[B0], on="sx")
-    km = ts(T.mk[96:128], T.nxr[96:128], float(me), A.not_equal, free=True, on="t2")
-    fill(T.rs[:], 1.0, on="sz")
-    cp(T.off1[:], T.io32[:, 0:4], free=True, on="sz", after=[("g1", 2)])
-    ts(rk[B0], T.tn[B0, :, 0], -127.75, A.add, 1.0 / 256, A.mult, after=[ktn])
-    ku = ts(mine[B0], T.tn[B0, :, 0], 2.0, A.mult, on="sx", after=[kmine])
+    kwb = ts(T.winb[:, 0:4], T.io4[:], goal, A.is_equal, on="*", after=[kgoal])
+    ts(new("q16"), T.p15[:], -15.5, A.add, on="sc")
+    ts(new("keep"), c("pp"), float(ID1), A.is_ge, c("le13"), A.mult, on="sd")
+    for h in range(2):
+        ku = cp(mine[B0, h:8:2], T.tn[B0, :, 16 * h], free=True, on="sp", after=[ktn, kmine])
+    kk = ts(new("keepr"), c("pp"), float(SENT), A.is_ge, c("le13"), A.mult, free=True, on="sd")
+    ends(me, "t2")
+    kslot = ts(T.slot3[:], T.io4[:, 0:3], -16.0, A.mult, c("q16"), A.subtract, on="sc")
+    for b in range(0, 96, 32):
+        ts(T.lists[b:b + 32, 40:48], mine[B0], -510.0, A.add, 1.0 / 1024, A.mult, free=True, after=[ku])
     to_rest([ku], 0, s.f1, lambda k: mine, T.fu[:])
     to_peer([ku], s.m1, lambda k: mine, mine)
+    column(me, "t2")
+    km = ts(T.mk[96:128], T.nxr[96:128], float(me), A.not_equal, free=True, on="t2")
 
-    wait(a, "a", "g2", 1)
-    level(T.d01[:], c("even"), free=True)
-    kw1 = act(new("init1"), T.ee[:, 3:4], scale=-272.0, bias=c("u1"))
-    for h in range(2):
-        kwme = act(T.win[:, 512 * me + h:512 * me + 512:2], T.io256[:], scale=e2(C1), bias=c("vme"), free=True, on="r3")
-    kvs1 = act(T.vs1[:], T.io256[:].indirect(qsel), C.Copy, free=True, on="*", after=[kq])
+    kv3 = act(T.v3[:], T.on3[:], bias=e2(ID1), free=True, after=[kon])
+    act(new("init2"), T.ee[:, PLACE:PLACE + 1], scale=-float(LAND + M), bias=c("u2"), on="sb")
+    wait(a, "a", *kv3)
     kreg = {}
     for k in (peer, 0, 1):
         for h in range(2):
-            kreg[k] = level(T.win[:, 512 * others[k] + 256 * h:512 * others[k] + 256 * h + 256], c("v%d" % k), free=True, on="r%d" % k)
-    act(new("keepo"), e2(N0), scale=-1.0, bias=c("keep"), free=True, on="sb", after=[kk])
-    act(new("u2"), c("pp"), scale=float(CAP), bias=-1.0 - CAP * SENT, free=True, on="sb")
-    act(T.bt0[:], T.io4[:], C.Copy, scale=e2(ID0), free=True, on="sb", after=[("g1", 2)])
-    level(T.data0[:, 0:512:128], c("keepr"), free=True, on="sb")
+            kreg[k] = level(T.win[:, 512 * others[k] + 256 * h:512 * others[k] + 256 * h + 256], T.v3[:, k:k + 1], free=True, on="r%d" % k)
+    kko = act(new("keepo"), e2(N0), scale=-1.0, bias=c("keep"), free=True, on="*", after=[kk])
+
+    cp(T.gg1[:], T.winb[:, 0:4].indirect(rk), after=[kwb])
+    for k in range(3):
+        km = ts(T.mk[32 * k:32 * k + 32], T.nxr[32 * k:32 * k + 32], float(others[k]), A.is_equal, free=True, on="t2")
+    ks1 = scan(T.gs1[:], T.d01[:], T.gg1[:], 0.0, after=[kone])
+    kxq = vec(v.quantize_mx, T.xq[:], T.xs[:], T.xb[:], free=True, on="*", after=[("dx", 16)])
+    for b in range(0, 128, 32):
+        kstu = cp(T.lists[b:b + 32, 48:56], T.stb[B0], free=True, on="sq", after=[("ds1", 32)])
+    kq = cp(qsel[B0], T.sth[B0, 0:8:2], free=True, on="*")
+    cp(T.offsel[:], T.io32[:], free=True, on="sf")
+    kp0 = cp(words(T.pk0[:]), words(T.xq[:]).indirect(stu), free=True, on="*", after=[kxq, kstu])
+    here = slice(512 * me, 512 * me + 512)
+    dma(a, T.win[GOES:GOES + 4, here], T.mk[:], "drow", after=[km, kwme])
+    dma(a, T.win[SENT:SENT + 3, here], T.mk[0:96], "drow")
+    dma(a, T.win[PLACE:PLACE + 4, here], T.gt[:, 16 * me:16 * me + 16], "drow")
+    for n in range(3):
+        kn = act(T.sg[:, 128 * n:128 * n + 128], T.gs1[:], C.Sign, bias=T.slot3[:, n:n + 1], accum_out=T.acc[:, n:n + 1], free=True, on="s4", after=[ks1, kslot])
+    ks0 = act(T.ps0[:], T.xs[:].indirect(stu), C.Copy, on="*", after=[kxq, kstu])
     for r in others:
-        level(T.data0[:, 128 * r + 1:128 * r + 128], c("keep"), free=True, on="sb")
-    level(T.data0[:, 128 * me + 1:128 * me + 128], c("keepo"), on="sb")
-    act(new("init2"), T.ee[:, PLACE:PLACE + 1], scale=-float(LAND + M), bias=c("u2"), free=True, on="sb")
+        level(T.data0[:, 128 * r + 1:128 * r + 128], c("keep"), free=True, on="se")
     for r in range(N):
         kw2 = act(T.bs[:, r:r + 1], e2(N0), scale=float(CAP * others.index(r) - LAND) if r != me else -1.0, bias=T.bt0[:, r:r + 1], free=True, on="sb")
-    kc0 = act(T.c0m[:], T.vs1[:], scale=e2(N0), bias=T.bs[:, me:me + 1], on="*", after=[kvs1, kw2])
-
-    fill(T.rs[:, 0:48:4], 0.0, free=False, on="sz")
-    fill(T.w1[:, 128:272], 0.0, on="sz")
-    cp(T.gg1[:], T.winb[:, 0:4].indirect(rk), after=[kw1])
-    cp(T.offsel[:], T.io32[:], free=True, on="sf")
-    cp(T.off2[:], T.io32[:], free=True, on="sf")
-    kso = fill(T.s2[:, 512:640], 0.0, on="sf")
-    scan(T.gs1[B0], T.d01[B0], T.gg1[B0], c("init1")[B0])
-    fill(T.rs7[:], 1.0, on="se")
-    turn(T.tg[B0], T.gs1[B0])
-    fill(T.rs7[:, 0:112:7], 0.0, free=False, on="se")
-    tt(T.x1[B0], T.tg[B0, :, 0:4], T.tg[B0, :, 16:20], A.mult)
-    kxq = vec(v.quantize_mx, T.xq[:], T.xs[:], T.xb[:], free=True, on="*", after=[("dx", 16)])
-    scan(T.y1[B0], T.rs[B0, 0:16], T.x1[B0], 0.0, after=[last("sz")])
-    ts(T.off1[B0], T.y1[B0, 3:16:4], 128.0, A.add)
+    for k in range(3):
+        ts(T.list1[B0, 3 * k:3 * k + 3], T.acc[32 * k:32 * k + 32], -0.5, A.mult, 64.0, A.add, free=k > 0, after=[kn])
+    ts(T.data0[:, 0:512:128], T.io256[:, 0:4], 0.0, A.mult, c("keepr"), A.add, free=True, on="s6", after=[kk])
+    kd0 = ts(T.data0[:, 128 * me + 1:128 * me + 128], T.io256[:, 0:127], 0.0, A.mult, c("keepo"), A.add, free=True, on="s6", after=[kko])
+    for b in range(32, 128, 32):
+        kl = cp(T.list1[b:b + 32, 0:9], T.list1[B0, 0:9], free=b > 32)
+    kul = fill(T.ul[:], 0, on="*")
     iota(T.w2[:, 0:M + LAND], [[0, M + LAND]], "g4")
-    cp(T.w1[:].indirect(T.off1[:]), T.vs1[:], after=[kvs1])
-    cp(T.d1[B0, 0:18:2, :], T.w1[B0, 128:272])
-    cp(T.d1[B0, 1:18:2, :], T.w1[B0, 128:272], free=True)
-    turn(T.td1[B0], T.d1[B0])
-    for b in range(2):
-        tt(T.l1f[32 * b:32 * b + 32], T.td1[B0, :, 0], T.td1[B0, :, 16], A.add, free=b > 0)
-    for b in range(2):
-        kl = ts(T.list1[64 * b:64 * b + 64, 0:9], T.l1f[0:64], -1.0, A.add, free=b > 0)
-    kpk = cp(words(T.pk1[:]), words(T.xq[:]).indirect(T.list1[:, 0:9]), after=[kxq])
-    ksc = act(T.ps1[:], T.xs[:].indirect(T.list1[:, 0:9]), C.Copy, on="*", after=[kl, kxq])
-    to_rest([kpk], 0, s.f1c, lambda k: raw(T.pk1[:, CAP * k:CAP * k + CAP]), raw(T.fc1[:]))
-    to_rest([ksc], 1, s.f1s, lambda k: T.ps1[:, CAP * k:CAP * k + CAP], T.fs1[:])
-    to_peer([kpk], s.c1, lambda k: raw(T.pk1[:, CAP * k:CAP * k + CAP]), raw(T.cb[:, CAP * at:CAP * at + CAP]))
-    to_peer([ksc], s.c1, lambda k: T.ps1[:, CAP * k:CAP * k + CAP], T.cbs[:, CAP * at:CAP * at + CAP])
+    ksc = act(T.ps1[:], T.ps0[:].indirect(T.list1[:, 0:9]), C.Copy, on="*", after=[kl, ks0])
 
-    here = slice(512 * me, 512 * me + 512)
-    dma(g.sync, T.win[GOES:GOES + 4, here], T.mk[:], "drow", after=[km, kwme])
-    dma(g.sync, T.win[SENT:SENT + 3, here], T.mk[0:96], "drow")
-    dma(g.sync, T.win[PLACE:PLACE + 4, here], T.gt[:, 16 * me:16 * me + 16], "drow")
-    dma(g.sync, T.wb[:], T.w[:], "dw")
-    for k in (peer, 0, 1):
-        there = slice(512 * others[k], 512 * others[k] + 512)
-        dma(g.sync, T.win[PLACE:PLACE + 4, there], T.gl[k], "drow", after=[kreg[k], ("m0%d" % k, 8)])
-        dma(g.sync, T.win[SLOT + k:SLOT + k + TWIN + 1:TWIN, there], T.gl[k, 0:64], "drow")
-    dma(g.sync, raw(T.cb[:, LAND:LAND + TX]), raw(T.xq[:]), "dcb", after=[kxq])
-    dma(g.sync, T.cbs[:, LAND:LAND + TX], T.xs[:], "dcb")
-    dma(g.sync, raw(T.lp[:, 96:176]), raw(T.xq[:, 0:80]), "dcb")
-    dma(g.sync, T.lps[:, 96:176], T.xs[:, 0:80], "dcb")
+    for ks in ([peer], rest):
+        for k in ks:
+            dma(g.sync, T.btr[B0, 8 * others[k]:8 * others[k] + 8], T.bl[k], "dbo", after=[("mb%d" % k, 1 if k == peer else 8)])
+        for k in ks:
+            there = slice(512 * others[k], 512 * others[k] + 512)
+            dma(g.sync, T.win[PLACE:PLACE + 4, there], T.gl[k], "drow", after=[kreg[k], ("m0%d" % k, 8 if k == peer else FEW)])
+        if peer in ks:
+            for k in (1, 0):
+                dma(g.sync, T.wb[:, 512 * k:512 * k + 512], T.w[:, 512 * k:512 * k + 512], "dw%d" % k)
 
-    ready = [("m1", 24), last("drow"), ku]
+    def again(codes, plane, at0, h):
+        return vec(v.quantize_mx, codes[:, at0:at0 + 128], plane[:, at0:at0 + 128], T.xb[:, 512 * h:512 * h + 512], free=True, on="s7")
+
+    tt(T.ux[B0], T.ulf[B0], T.btr[B0], A.add, on="s5", after=[ku, ("m1", 24), last("dbo")])
+    kso = fill(T.s2[:, 512:640], 0.0, on="sf")
+    fill(T.rs7[:], 1.0, on="sz")
+    ready = [ts(T.ul[B0], T.ux[B0], 0.5, A.mult, -0.25, A.add, on="s5", after=[kul]), last("drow")]
+    ko2 = cp(T.off2[:], T.io32[:], free=True, on="*")
+    fill(T.rs7[:, 0:112:7], 0.0, free=False, on="sz")
+    keven = ts(new("even"), p, 16.0, A.is_lt, free=True, on="*")
     kgb = act(T.g2[:, 256:512], T.win[:].indirect(T.ul[:, 16:32]), C.Copy, on="sa", after=ready)
+    kvs1 = act(T.vs1[:], T.io256[:].indirect(qsel), C.Copy, free=True, on="*", after=[kq])
+    kc0 = act(T.c0m[:], T.vs1[:], scale=e2(N0), bias=T.bs[:, me:me + 1], on="*", after=[kvs1, kw2])
     cp(T.g2[:, 0:256], T.win[:].indirect(T.ul[:, 0:16]), on="sx", after=ready)
-    ks = scan(T.s2[:, 0:512], T.data0[:], T.g2[:], c("init2"), on="sx", after=[kgb, kw2])
+    kpk = cp(words(T.pk1[:]), words(T.pk0[:]).indirect(T.list1[:, 0:9]), after=[kp0])
+    to_rest([ksc, last("drow"), last("dbo")], 0, s.f1s, lambda k: T.ps1[:, CAP * k:CAP * k + CAP], T.fs1[:])
+    to_peer([ksc], s.c1, lambda k: T.ps1[:, CAP * k:CAP * k + CAP], T.cbs[:, CAP * at:CAP * at + CAP])
+    to_rest([kpk], 0, s.f1c, lambda k: raw(T.pk1[:, CAP * k:CAP * k + CAP]), raw(T.fc1[:]))
+    to_peer([kpk], s.c1, lambda k: raw(T.pk1[:, CAP * k:CAP * k + CAP]), raw(T.cb[:, CAP * at:CAP * at + CAP]))
+    ks = scan(T.s2[:, 0:512], T.data0[:], T.g2[:], c("init2"), on="sx", after=[kgb, kw2, kd0, last("se")])
     for n, r in enumerate(others):
         kvsel = act(T.vsel[:, 64 * r:64 * r + 64], T.s2[:].indirect(T.offsel[:, 4 * r:4 * r + 4]), bias=T.bs[:, r:r + 1], free=n > 0, on="sa", after=[ks, kso])
+    kq2 = quant(2)
     turn(T.tg2[B0], T.s2[B0, 0:512], on="sx")
     tt(T.vsel[:, 64 * me:64 * me + 64], T.s2[:].indirect(T.offsel[:, 4 * me:4 * me + 4]), T.c0m[:], A.add, free=True, on="so", after=[kso, kc0])
     for k in range(3):
@@ -354,10 +369,11 @@ def rank_program(g, core, T, topo):
     tt(T.x2[B0, 3:112:7], T.tg2[B0, :, PLACE], T.tg2[B0, :, ENDS], A.mult, free=True, on="sx")
     tt(T.x2[B0, 4:112:7], T.tg2[B0, :, ENDS], T.ntr[B0], A.mult, free=True, on="sx", after=[("g3", 2)])
     tt(T.x2[B0, 5:112:7], T.tg2[B0, :, LEAVES], T.ntr[B0], A.mult, free=True, on="sx")
-    scan(T.y2[B0], T.rs7[B0], T.x2[B0], 0.0, on="sx", after=[last("se")])
-    kq2 = quant(2)
-    ts(T.off2[B0], T.y2[B0, 6:112:7], float(M), A.add, on="sx")
+    again(T.cb, T.cbs, LAND, 0)
+    scan(T.y2[B0], T.rs7[B0], T.x2[B0], 0.0, on="sx", after=[last("sz")])
     kq1 = quant(1)
+    ts(T.off2[B0], T.y2[B0, 6:112:7], float(M), A.add, on="sx", after=[ko2])
+    kcb = again(T.cb, T.cbs, LAND + 128, 1)
     kw = cp(T.w2[:].indirect(T.off2[:]), T.vsel[:], on="sx", after=[last("so"), kvsel, ("g4", 1)])
     kwq = quant(0)
     wait(v, "v", *kw)
@@ -366,20 +382,26 @@ def rank_program(g, core, T, topo):
         return T.wq[:, 128 * k:128 * k + 128], T.ws[:, 128 * k:128 * k + 128]
     m2 = mm(T.ps[:, 1024:1280], *w(2), T.xq[:], T.xs[:], True, True, free=True, after=[kq2, kxq])
     m1 = mm(T.ps[:, 512:768], *w(1), T.xq[:], T.xs[:], True, True, after=[kq1])
-    m0 = mm(T.ps[:, 0:400], *w(0), T.cb[:], T.cbs[:], True, True, after=[kwq, ("c1", 48), last("dcb")])
+    m0 = mm(T.ps[:, 0:400], *w(0), T.cb[:], T.cbs[:], True, True, after=[kwq, ("c1", 48), kcb])
     for x, at0 in ((T.aw, LAND), (T.bw, 0), (T.cw, 0)):
         level(x[:, at0:at0 + 1], 0.0, free=True, on="sb")
-    act(new("idb"), c("even"), C.Copy, scale=-1.0, free=True, on="sb")
+    act(new("idb"), c("even"), C.Copy, scale=-1.0, free=True, on="sb", after=[keven])
+    act(new("s2"), e2(SLOT), bias=e2(SLOT + 1), free=True, on="s3")
+    act(new("u3"), p, scale=float(CAP), bias=-1.0 - LAND - CAP * SLOT, free=True, on="s3")
+    act(new("s3"), e2(SLOT + 2), bias=c("s2"), on="s3")
+    act(new("init3"), c("u3"), C.Copy, scale=c("even"), free=True, on="s3")
+    k3 = level(T.data3[:], c("s3"), on="s3")
     act(T.cw[:, 1:257], T.ps[:, 1024:1280], C.Copy, free=True, on="sb", after=[m2])
     kbw = act(T.bw[:, 1:257], T.ps[:, 512:768], C.Copy, free=True, on="sb", after=[m1])
     kid = act(T.idl[:], T.w2[:, 0:M], bias=c("idb"), on="sk", after=[kw, kbw])
     dma(g.sync, T.id[:], T.idl[ID0:ID0 + 2, :], "did", after=[kid])
 
-    cp(T.d2[B0, 0:18:2, :], T.w2[B0, M:M + LAND], after=[kpk])
+    cp(T.d2[B0, 0:18:2, :], T.w2[B0, M:M + LAND])
     cp(T.d2[B0, 1:18:2, :], T.w2[B0, M:M + LAND], free=True)
-    cp(T.dp[B0, 0:24:2, :], T.w2[B0, 0:M], free=True, on="sd")
+    scan(T.w3[B0], T.data3[B0], T.w2[B0, 0:M], c("init3")[B0], free=True, on="sd", after=[k3])
     turn(T.td2[B0], T.d2[B0])
-    cp(T.dp[B0, 1:24:2, :], T.w2[B0, 0:M], free=True, on="sd")
+    cp(T.dp[B0, 0:24:2, :], T.w3[B0], on="sd")
+    cp(T.dp[B0, 1:24:2, :], T.w3[B0], free=True, on="sd")
     for b in range(2):
         for h, r in enumerate((N0, C1)):
             tt(T.nf[32 * b:32 * b + 32, :, h, :], T.td2[B0, :, :, r], T.td2[B0, :, :, TWIN + r], A.add, free=b + h > 0)
@@ -388,13 +410,13 @@ def rank_program(g, core, T, topo):
         kl2 = ts(T.list2[64 * b:64 * b + 64], T.nf[0:64], LAND - 1.0, A.add, free=b > 0)
     tt(T.qz[B0, 0:12], T.tp[B0, :, C1], T.tp[B0, :, TWIN + C1], A.add, on="sd")
     tt(T.qz[B0, 12:24], T.tp[B0, :, C2], T.tp[B0, :, C2 + 1], A.add, free=True, on="sd")
-    landed = [("c1", 48), last("dcb")]
+    landed = [("c1", 48), kcb]
     ksa = act(T.ps2[:, 0:192], T.cbs[:].indirect(T.list2[:, 0:12]), C.Copy, on="sa", after=[kl2] + landed)
     ksb = act(T.ps2[:, 192:288], T.cbs[:].indirect(T.list2[:, 12:18]), C.Copy, on="*")
     kpa = cp(words(T.pk2[:, 0:192]), words(T.cb[:]).indirect(T.list2[:, 0:12]), after=landed)
     kpb = cp(words(T.pk2[:, 192:288]), words(T.cb[:]).indirect(T.list2[:, 12:18]), free=True, on="so")
     to_rest([kpa], 0, s.f2c, lambda k: raw(T.pk2[:, 96 * k:96 * k + 96]), raw(T.fc2[:]))
-    to_rest([ksa], 1, s.f2s, lambda k: T.ps2[:, 96 * k:96 * k + 96], T.fs2[:])
+    to_rest([ksa], 0, s.f2s, lambda k: T.ps2[:, 96 * k:96 * k + 96], T.fs2[:])
     to_peer([kpb], s.c2p, lambda k: raw(T.pk2[:, 96 * k:96 * k + 96]), raw(T.lp[:, 0:96]))
     to_peer([ksb], s.c2p, lambda k: T.ps2[:, 96 * k:96 * k + 96], T.lps[:, 0:96])
     g.wait_ge(s.did, 16)
@@ -403,19 +425,22 @@ def rank_program(g, core, T, topo):
     tt(T.z3[B0], T.tp[B0, :, N0], T.tp[B0, :, TWIN + N0], A.add, free=True, on="sd")
     tt(T.fl[B0, :, 0:3], T.tp[B0, :, ON:ON + 3], T.tp[B0, :, TWIN + ON:TWIN + ON + 3], A.add, free=True, on="sd")
     tt(T.x3[B0, :, 0:3], T.tp[B0, :, SLOT:SLOT + 3], T.tp[B0, :, TWIN + SLOT:TWIN + SLOT + 3], A.add, free=True, on="sd")
+    fill(T.rs[:], 1.0, on="sz")
+    klp = vec(v.quantize_mx, T.lp[:, 96:224], T.lps[:, 96:224], T.xb[:, 0:512], free=True, on="*")
     ts(T.fl[B0, :, 3], T.qz[B0, 0:12], 1.0, A.min, on="sd")
     ts(T.x3[B0, :, 3], T.z3[B0], float(LAND), A.add, free=True, on="sd")
     for b in range(0, 128, 32):
         kqbc = cp(T.qbc[b:b + 32], T.qz[B0], free=True, on="sc")
     tt(T.x3m[B0], T.x3[B0], T.fl[B0], A.mult, on="sd")
+    fill(T.rs[:, 0:48:4], 0.0, free=False, on="sz")
     kaw = act(T.aw[:, LAND + 1:LAND + 401], T.ps[:, 0:400], C.Copy, free=True, on="sb", after=[m0])
     kt1 = act(T.t1[:], T.cw[:, 0:257].indirect(T.qbc[:, 12:24]), C.Copy, on="sa", after=[kqbc, kbw])
-    scan(T.y4[B0], T.rs[B0], T.x3m[B0], 0.0, on="sd")
+    scan(T.y4[B0], T.rs[B0], T.x3m[B0], 0.0, on="sd", after=[last("sz")])
     for b in range(0, 128, 32):
         kq0 = ts(T.q0[b:b + 32], T.y4[B0, 3:48:4], float(LAND), A.add, free=b > 0, on="sd")
     tt(T.t2[:], T.bw[:, 0:257].indirect(T.qbc[:, 0:12]), T.t1[:], A.add, on="so", after=[kqbc, kt1])
 
-    mm(T.ps[:, 2048:2176], *w(0), T.lp[:, 0:128], T.lps[:, 0:128], True, False, after=[("c2p", 16)])
+    mm(T.ps[:, 2048:2176], *w(0), T.lp[:, 0:128], T.lps[:, 0:128], True, False, after=[klp, ("c2p", 16)])
     mp = mm(T.ps[:, 2048:2176], *w(1), T.lp[:, 48:176], T.lps[:, 48:176], False, True, free=True)
     mm(T.ps[:, 1536:1680], *w(0), T.lr[:, 0:144], T.lrs[:, 0:144], True, False, after=[("c2", 32)])
     mr = mm(T.ps[:, 1536:1680], *w(1), T.lr[:, 48:192], T.lrs[:, 48:192], False, True, free=True)

from concourse.bass import DstId, RemoteDMATransfer
from concourse.mybir import dt, AluOpType, ActivationFunctionType

N, CAP, TX, M = 4, 48, 256, 192
LAND = 3 * CAP
F, B, I, U = "float32", "bfloat16", "int32", "uint16"
CODE, PLANE = "float8_e4m3fn_x4", "uint8"
ON, SLOT, C1, ID0, ID1, N0, SENT, PLACE, ENDS, C2, GOES, LEAVES = 0, 3, 6, 7, 8, 9, 10, 13, 14, 15, 17, 20
PAIRED, TWIN = 10, 22
FEW = 2


def _sb(d, *s):
    return ("sbuf", [128] + list(s), d)


SCRATCH = {
    "xb": _sb(B, 1024), "wb": _sb(B, 1536),
    "xq": _sb(CODE, 256), "xs": _sb(PLANE, 256), "cb": _sb(CODE, 400), "cbs": _sb(PLANE, 400), "wq": _sb(CODE, 384), "ws": _sb(PLANE, 384),
    "pk1": _sb(CODE, 144), "ps1": _sb(PLANE, 144), "pk2": _sb(CODE, 288), "ps2": _sb(PLANE, 288),
    "fc1": _sb(CODE, 48), "fs1": _sb(PLANE, 48), "fc2": _sb(CODE, 96), "fs2": _sb(PLANE, 96),
    "fu": _sb(F, 8), "fn": ("dram", [128, 16], B), "gt": _sb(B, 64), "gl": ("dram", [3, 128, 16], B),
    "lr": _sb(CODE, 192), "lrs": _sb(PLANE, 192), "lp": _sb(CODE, 224), "lps": _sb(PLANE, 224),
    "pmi": _sb(F, 32), "ee": _sb(F, 32), "e2": _sb(F, 10), "e16": _sb(F, 4), "col": _sb(F, 32), "io32": _sb(I, 16), "io4": _sb(F, 4),
    "io256": _sb(B, 256), "d01": _sb(B, 128), "offsel": _sb(U, 16), "ntr": _sb(F, 16), "data0": _sb(B, 512),
    "rs": _sb(F, 48), "rs7": _sb(F, 112), "btl": ("dram", [128, 2], I), "fb": ("dram", [128, 2], I), "bl": ("dram", [3, 128, 2], I),
    "btr": _sb(I, 32), "ulf": _sb(F, 32), "ux": _sb(F, 32),
    "data3": _sb(B, 192), "w3": _sb(B, 192), "on3": _sb(F, 3), "v3": _sb(F, 3),
    "winb": _sb(B, 16), "bs": _sb(F, 4), "bt0": _sb(F, 4),
    "stb": _sb(I, 8), "b0": _sb(I, 4), "sx": _sb(I, 4), "sy": _sb(I, 4), "sz": _sb(I, 4), "sw": _sb(I, 4),
    "lists": _sb(U, 64), "p1w": _sb(I, 512), "nd": _sb(F, 128), "tn": _sb(F, 4, 32), "ul": _sb(U, 32),
    "nxs": _sb(I, 32), "nxt": _sb(I, 32), "nxr": _sb(I, 16), "mk": _sb(B, 16), "win": _sb(B, 2048),
    "gg1": _sb(B, 128), "gs1": _sb(B, 128), "sg": _sb(B, 384), "acc": _sb(F, 3), "slot3": _sb(F, 3), "p15": _sb(I, 1), "sth": _sb(I, 16),
    "vs1": _sb(B, 64), "c0m": _sb(B, 64), "list1": _sb(U, 10), "pk0": _sb(CODE, 144), "ps0": _sb(PLANE, 144),
    "g2": _sb(B, 512), "s2": _sb(B, 640), "tg2": _sb(B, 16, 32), "x2": _sb(F, 112), "y2": _sb(F, 112), "off2": _sb(U, 16),
    "vsel": _sb(B, 256), "w2": _sb(B, 848), "d2": _sb(B, 18, 16), "td2": _sb(B, 3, 3, 32), "nf": _sb(F, 3, 2, 3), "list2": _sb(U, 18),
    "idl": _sb(F, 192), "dp": _sb(B, 24, 16), "tp": _sb(B, 12, 32), "fl": _sb(F, 12, 4), "x3": _sb(F, 12, 4), "z3": _sb(F, 12), "qz": _sb(F, 24),
    "x3m": _sb(F, 48), "y4": _sb(F, 48), "q0": _sb(U, 12), "qbc": _sb(U, 24),
    "ps": ("psum", [128, 2560], F), "aw": _sb(F, 552), "bw": _sb(F, 264), "cw": _sb(F, 264),
    "t1": _sb(F, 192), "t2": _sb(F, 192), "yo": _sb(F, 192),
}
SINGLE = ["k%d" % n for n in range(32)]
CHAINS = ["sv", "su", "so", "sz", "sq", "sc", "sd", "se", "sf", "sa", "sb", "sk", "sp", "st", "sx", "s3", "s4", "s5", "s6", "s7", "s8", "t0", "t1", "t2", "r0", "r1", "r2", "r3"] + SINGLE
SEMAPHORES = CHAINS + ["g0", "g1", "g2", "g3", "g4", "dbl", "dbo", "fb", "mb0", "mb1", "mb2", "dst", "dbt", "ds1", "dnx", "dns", "dx", "dw0", "dw1", "dw2", "drow", "dy", "did", "dia",
                       "m00", "m01", "m02", "m1", "c1", "c2", "c2p", "loc", "f0", "f1", "f1c", "f1s", "f2c", "f2s"]


def order(topo, cores, r):
    return sorted([k for k in range(N) if k != r], key=lambda k: topo.may_write(cores[r], cores[k]))


def forwarders(topo, src, dst):
    near = topo.host(src) == topo.host(dst)
    return [k for k in topo.cores_of(src) if topo.may_write(k, dst) and (topo.die(k) == topo.die(src)) == near][:2]


def mask_of(engines):
    return sum(1 << e for e in engines)


def hand_on(g, core, T, topo):
    for i, src in enumerate(T.cores):
        for j, dst in enumerate(T.cores):
            if i == j or topo.may_write(src, dst) or core not in forwarders(topo, src, dst):
                continue
            h = forwarders(topo, src, dst).index(core)
            k = order(topo, T.cores, j).index(i)
            rid, pid = topo.addr(dst, core)
            e = topo.engines(core, dst)
            s = T.sem
            half = len(topo.engines(src, core)) // 2
            if h:
                continue
            jobs = [(s.fb, 1, e, T.bl[k], T.fb[:], s["mb%d" % k]),
                    (s.f0, half // 2, e[:FEW], T.gl[k], T.fn[:], s["m0%d" % k]),
                    (s.f1, half, e, T.ulf[:, 8 * i:8 * i + 8], T.fu[:], s.m1),
                    (s.f1s, half, e, T.cbs[:, CAP * k:CAP * k + CAP], T.fs1[:], s.c1),
                    (s.f1c, half, e, T.cb[:, CAP * k:CAP * k + CAP].bitcast(dt.uint8), T.fc1[:].bitcast(dt.uint8), s.c1),
                    (s.f2c, half, e, T.lr[:, 96 * k:96 * k + 96].bitcast(dt.uint8), T.fc2[:].bitcast(dt.uint8), s.c2),
                    (s.f2s, half, e, T.lrs[:, 96 * k:96 * k + 96], T.fs2[:], s.c2)]
            for sem, n, use, out, in_, to in jobs:
                g.wait_ge(sem, n)
                g.remote_dma(out, in_, to, s.loc, pid, rid, mask_of(use))
            g.wait_ge(s.loc, sum(len(job[2]) for job in jobs))


def rank_program(g, core, T, topo):
    me = T.rank_of(core)
    if me is None:
        hand_on(g, core, T, topo)
        return
    A, C = AluOpType, ActivationFunctionType
    others = order(topo, T.cores, me)
    s, v, a = T.sem, g.vector, g.scalar
    cnt = {}
    known = {}

    def wait(q, name, sem, n):
        if known.get((name, sem), 0) < n:
            q.wait_ge(s[sem], n)
            known[(name, sem)] = n

    def put(q, name, chain, free, after, f, *args, **kw):
        if chain == "*":
            chain = [x for x in SINGLE if x not in cnt][0]
        for sem, n in after:
            wait(q, name, sem, n)
        if not free:
            wait(q, name, chain, cnt.get(chain, 0))
        f(*args, **kw).then_inc(s[chain], 1)
        cnt[chain] = cnt.get(chain, 0) + 1
        return (chain, cnt[chain])

    def last(chain):
        return (chain, cnt[chain])

    def vec(f, *args, free=False, on="sv", after=()):
        return put(v, "v", on, free, after, f, *args)

    def act(out, in_, func=C.Identity, free=False, on="sk", after=(), **kw):
        return put(a, "a", on, free, after, a.activation, out, in_, func, **kw)

    def mm(*args, free=False, after=()):
        return put(g.tensor, "t", "st", free, after, g.tensor.matmul_mx, *args)

    def ts(out, in_, s1, op0, s2=None, op1=None, **kw):
        if op1 is None:
            return vec(v.tensor_scalar, out, in_, s1, None, op0, **kw)
        return vec(v.tensor_scalar, out, in_, s1, s2, op0, op1, **kw)

    def tt(out, x, y, op, **kw):
        return vec(v.tensor_tensor, out, x, y, op, **kw)

    def cp(out, in_, **kw):
        return vec(v.tensor_copy, out, in_, **kw)

    def turn(out, in_, **kw):
        return vec(v.transpose, out, in_, **kw)

    def fill(out, x, free=True, on="so"):
        return vec(v.memset, out, x, free=free, on=on)

    def scan(out, d0, d1, init, **kw):
        return vec(v.tensor_tensor_scan, out, d0, d1, init, A.mult, A.add, **kw)

    def quant(k):
        return vec(v.quantize_mx, T.wq[:, 128 * k:128 * k + 128], T.ws[:, 128 * k:128 * k + 128], T.wb[:, 512 * k:512 * k + 512], free=True, on="*",
                   after=[("dw%d" % k, 16)])

    def dma(q, out, in_, sem, after=()):
        for x in after:
            wait(q, "s" if q is g.sync else "a", *x)
        q.dma_start(out, in_).then_inc(s[sem], 16)
        cnt[sem] = cnt.get(sem, 0) + 16

    def iota(out, pattern, sem, base=0, by=0):
        g.iota(out, pattern, base, by, allow_small_or_imprecise_dtypes=True).then_inc(s[sem], 1)

    def level(out, x, **kw):
        return act(out, T.io256[:, 0:out.shape[1]], scale=0.0, bias=x, **kw)

    def words(x):
        return x.bitcast(dt.uint32)

    def raw(x):
        return x.bitcast(dt.uint8)

    rest, peer = [0, 1], 2
    at = order(topo, T.cores, others[peer]).index(me)

    def call(after, items):
        for x in after:
            wait(g, "g", *x)
        tr = []
        for d, n, of, sem, src, dst in items:
            e = topo.engines(core, d)
            h = len(e) // of
            rid, pid = topo.addr(d, core)
            tr.append(RemoteDMATransfer(dst_ids=[DstId(rid=rid, pnc=pid)], dma_engine_mask=mask_of(e[n * h:n * h + h]), remote_sem=sem, src=src, dst=dst))
            cnt["loc"] = cnt.get("loc", 0) + h
        g.remote_dma_fused(tr, local_sem=s.loc)

    def to_rest(after, h, sem, src, held):
        call(after, [(forwarders(topo, core, T.cores[others[k]])[h], k, 2, sem, src(k), held) for k in rest])

    def to_peer(after, sem, src, lands):
        call(after, [(T.cores[others[peer]], 0, 1, sem, src(peer), lands)])

    col = {}

    def new(name):
        col[name] = T.col[:, len(col):len(col) + 1]
        return col[name]

    def c(name):
        return col[name]

    def e2(r):
        return T.e2[:, r:r + 1]

    G0, B0 = slice(0, 16), slice(0, 32)
    q1l, qsel, rk, stu = T.lists[:, 0:8], T.lists[:, 32:36], T.lists[:, 40:48], T.lists[:, 48:57]
    mine = T.ulf[:, 8 * me:8 * me + 8]

    for h, q in enumerate((g.sync, a)):
        dma(q, T.btl[64 * h:64 * h + 64, :], T.bt[:], "dbl")
    for h in range(2):
        dma(g.sync, T.sth[16 * h:16 * h + 16, 0:8 - h], T.st[:, h:8], "dst")
        dma(a, T.sth[16 * h:16 * h + 16, 8:16 - h], T.bt[:, h:8], "dbt")
    for b in range(0, 128, 32):
        dma(g.sync if b < 64 else a, T.nxs[b + 16:b + 32, :], T.nx[:], "dns")
    for h in range(2):
        dma(a, T.stb[16 * h:16 * h + 16, :], T.st[:], "ds1")
    kp = fill(T.p1w[:], 0, on="*")
    for h, q in enumerate((g.sync, a)):
        dma(q, T.p1w[16 * h:16 * h + 1, :], T.nx[:], "dnx", after=[kp])
    dma(g.sync, T.xb[:], T.x[:], "dx")
    dma(g.sync, T.wb[:, 1024:1536], T.w[:, 1024:1536], "dw2")
    iota(T.pmi[:], [[-1, 32]], "g0", by=1)
    dma(g.sync, T.btr[B0, 8 * me:8 * me + 8], T.btl[:], "dbo", after=[last("dbl")])
    iota(T.io256[:], [[1, 256]], "g2", base=1)
    call([last("dbl")], [(forwarders(topo, core, T.cores[others[k]])[0], 14 + k, 16, s.fb, T.btl[:], T.fb[:]) for k in rest]
         + [(T.cores[others[peer]], 0, 8, s["mb%d" % at], T.btl[:], T.bl[at])])
    g.iota(T.io32[:], [[32, 16]], 0, 1).then_inc(s.g1, 1)
    iota(T.io4[:], [[1, 4]], "g1", base=1)
    iota(T.ntr[:], [[-32, 16]], "g3", base=-LAND, by=-1)
    iota(T.x2[:, 6:112:7], [[32, 16]], "g3", base=LAND, by=1)

    p = T.pmi[:, 0:1]
    ts(T.ee[:], T.pmi[:], 0.0, A.is_equal, on="sc", after=[("g0", 1)])
    ts(new("m22"), p, float(TWIN), A.is_ge, -float(TWIN), A.mult, free=True, on="sc")
    for b in range(0, 128, 32):
        fill(T.nxs[b:b + 16, :], 0, on="su")
    klists = fill(T.lists[:], 0, on="*")
    tt(T.e2[:], T.ee[:, 0:PAIRED], T.ee[:, TWIN:TWIN + PAIRED], A.add, on="sc")
    ke = tt(new("pp"), p, c("m22"), A.add, free=True, on="sc")

    def column(e, on):
        return ts(T.gt[64:128, 16 * e:16 * e + 16], T.nxt[64:128, 16:32], 1.0 - 256.0 * e, A.add, free=True, on=on)

    def ends(e, on):
        return ts(T.gt[0:64, 16 * e:16 * e + 16], T.nxr[0:64], float(e), A.is_equal, free=True, on=on, after=[kr])
    ts(T.sx[B0], T.sth[B0, 0:8:2], 513.0, A.mult, free=True, on="sx", after=[("dst", 32)])
    ts(T.b0[B0], T.sth[B0, 8:16:2], 32.0, A.mult, free=True, on="sx", after=[("dbt", 32)])
    kon = tt(T.on3[:], T.e2[:, ON:ON + 3], T.e2[:, SLOT:SLOT + 3], A.add, free=True, on="*", after=[ke])
    turn(T.nxt[:], T.nxs[:], on="su", after=[("dns", 64)])
    ts(T.sw[B0], T.sx[B0], 3, A.logical_shift_right, 511, A.bitwise_and, on="sx")
    ts(T.sy[B0], T.b0[B0], 32, A.bitwise_and, free=True, on="sx")
    kr = ts(T.nxr[:], T.nxt[:, 16:32], 8, A.logical_shift_right, on="su")
    column(others[0], "t0")
    tt(T.sz[B0], T.sw[B0], T.sy[B0], A.add, on="sx")
    column(others[1], "t0")
    for k in rest:
        ends(others[k], "t0")
    cp(q1l[B0, 0:8:2], T.sz[B0], on="sx", after=[klists])
    cp(q1l[B0, 1:8:2], T.sz[B0], free=True, on="sx")
    ends(others[peer], "t1")
    column(others[peer], "t1")
    wait(a, "a", *ke)
    wait(a, "a", "g2", 1)
    kvme = act(new("vme"), e2(ID1), bias=e2(N0), free=True, on="*")
    goal = new("goal")
    for k, r in enumerate(others + [me]):
        kgoal = act(goal[32 * k:32 * k + 32], T.io256[32 * k:32 * k + 32, 0:1], scale=0.0, bias=r + 1.0, free=True, on="s8")
    kone = level(T.d01[:], 1.0, free=True, on="*")
    act(new("u2"), c("pp"), scale=float(CAP), bias=-1.0 - CAP * SENT, free=True, on="sb")
    act(T.bt0[:], T.io4[:], C.Copy, scale=e2(ID0), free=True, on="sb", after=[("g1", 2)])
    for h in range(2):
        kwme = act(T.win[:, 512 * me + h:512 * me + 512:2], T.io256[:], scale=e2(C1), bias=c("vme"), free=True, on="r3", after=[kvme])
    ts(T.nd[:], T.p1w[:].indirect(q1l), 4.0, A.mult, on="sx", after=[("dnx", 32)])
    call([last("t0")], [(forwarders(topo, core, T.cores[others[k]])[0], 2 + k, 4, s.f0, T.gt[:, 16 * others[k]:16 * others[k] + 16], T.fn[:]) for k in rest])
    to_peer([last("t1")], s["m0%d" % at], lambda k: T.gt[:, 16 * others[k]:16 * others[k] + 16], T.gl[at])
    kmine = fill(mine, 0.0, on="*")
    ts(T.p15[:], T.io32[:, 0:1], 15, A.bitwise_and, on="sc", after=[("g1", 2)])
    ts(new("le13"), c("pp"), PLACE + 0.5, A.is_lt, free=True, on="sd")
    ktn = turn(T.tn[B0], T.nd[B0], on="sx")
    kwb = ts(T.winb[:, 0:4], T.io4[:], goal, A.is_equal, on="*", after=[kgoal])
    ts(new("q16"), T.p15[:], -15.5, A.add, on="sc")
    ts(new("keep"), c("pp"), float(ID1), A.is_ge, c("le13"), A.mult, on="sd")
    for h in range(2):
        ku = cp(mine[B0, h:8:2], T.tn[B0, :, 16 * h], free=True, on="sp", after=[ktn, kmine])
    kk = ts(new("keepr"), c("pp"), float(SENT), A.is_ge, c("le13"), A.mult, free=True, on="sd")
    ends(me, "t2")
    kslot = ts(T.slot3[:], T.io4[:, 0:3], -16.0, A.mult, c("q16"), A.subtract, on="sc")
    for b in range(0, 96, 32):
        ts(T.lists[b:b + 32, 40:48], mine[B0], -510.0, A.add, 1.0 / 1024, A.mult, free=True, after=[ku])
    to_rest([ku], 0, s.f1, lambda k: mine, T.fu[:])
    to_peer([ku], s.m1, lambda k: mine, mine)
    column(me, "t2")
    km = ts(T.mk[96:128], T.nxr[96:128], float(me), A.not_equal, free=True, on="t2")

    kv3 = act(T.v3[:], T.on3[:], bias=e2(ID1), free=True, after=[kon])
    act(new("init2"), T.ee[:, PLACE:PLACE + 1], scale=-float(LAND + M), bias=c("u2"), on="sb")
    wait(a, "a", *kv3)
    kreg = {}
    for k in (peer, 0, 1):
        for h in range(2):
            kreg[k] = level(T.win[:, 512 * others[k] + 256 * h:512 * others[k] + 256 * h + 256], T.v3[:, k:k + 1], free=True, on="r%d" % k)
    kko = act(new("keepo"), e2(N0), scale=-1.0, bias=c("keep"), free=True, on="*", after=[kk])

    cp(T.gg1[:], T.winb[:, 0:4].indirect(rk), after=[kwb])
    for k in range(3):
        km = ts(T.mk[32 * k:32 * k + 32], T.nxr[32 * k:32 * k + 32], float(others[k]), A.is_equal, free=True, on="t2")
    ks1 = scan(T.gs1[:], T.d01[:], T.gg1[:], 0.0, after=[kone])
    kxq = vec(v.quantize_mx, T.xq[:], T.xs[:], T.xb[:], free=True, on="*", after=[("dx", 16)])
    for b in range(0, 128, 32):
        kstu = cp(T.lists[b:b + 32, 48:56], T.stb[B0], free=True, on="sq", after=[("ds1", 32)])
    kq = cp(qsel[B0], T.sth[B0, 0:8:2], free=True, on="*")
    cp(T.offsel[:], T.io32[:], free=True, on="sf")
    kp0 = cp(words(T.pk0[:]), words(T.xq[:]).indirect(stu), free=True, on="*", after=[kxq, kstu])
    here = slice(512 * me, 512 * me + 512)
    dma(a, T.win[GOES:GOES + 4, here], T.mk[:], "drow", after=[km, kwme])
    dma(a, T.win[SENT:SENT + 3, here], T.mk[0:96], "drow")
    dma(a, T.win[PLACE:PLACE + 4, here], T.gt[:, 16 * me:16 * me + 16], "drow")
    for n in range(3):
        kn = act(T.sg[:, 128 * n:128 * n + 128], T.gs1[:], C.Sign, bias=T.slot3[:, n:n + 1], accum_out=T.acc[:, n:n + 1], free=True, on="s4", after=[ks1, kslot])
    ks0 = act(T.ps0[:], T.xs[:].indirect(stu), C.Copy, on="*", after=[kxq, kstu])
    for r in others:
        level(T.data0[:, 128 * r + 1:128 * r + 128], c("keep"), free=True, on="se")
    for r in range(N):
        kw2 = act(T.bs[:, r:r + 1], e2(N0), scale=float(CAP * others.index(r) - LAND) if r != me else -1.0, bias=T.bt0[:, r:r + 1], free=True, on="sb")
    for k in range(3):
        ts(T.list1[B0, 3 * k:3 * k + 3], T.acc[32 * k:32 * k + 32], -0.5, A.mult, 64.0, A.add, free=k > 0, after=[kn])
    ts(T.data0[:, 0:512:128], T.io256[:, 0:4], 0.0, A.mult, c("keepr"), A.add, free=True, on="s6", after=[kk])
    kd0 = ts(T.data0[:, 128 * me + 1:128 * me + 128], T.io256[:, 0:127], 0.0, A.mult, c("keepo"), A.add, free=True, on="s6", after=[kko])
    for b in range(32, 128, 32):
        kl = cp(T.list1[b:b + 32, 0:9], T.list1[B0, 0:9], free=b > 32)
    kul = fill(T.ul[:], 0, on="*")
    iota(T.w2[:, 0:M + LAND], [[0, M + LAND]], "g4")
    ksc = act(T.ps1[:], T.ps0[:].indirect(T.list1[:, 0:9]), C.Copy, on="*", after=[kl, ks0])

    for ks in ([peer], rest):
        for k in ks:
            dma(g.sync, T.btr[B0, 8 * others[k]:8 * others[k] + 8], T.bl[k], "dbo", after=[("mb%d" % k, 1 if k == peer else 8)])
        for k in ks:
            there = slice(512 * others[k], 512 * others[k] + 512)
            dma(g.sync, T.win[PLACE:PLACE + 4, there], T.gl[k], "drow", after=[kreg[k], ("m0%d" % k, 8 if k == peer else FEW)])
        if peer in ks:
            for k in (1, 0):
                dma(g.sync, T.wb[:, 512 * k:512 * k + 512], T.w[:, 512 * k:512 * k + 512], "dw%d" % k)

    def again(codes, plane, at0, h):
        return vec(v.quantize_mx, codes[:, at0:at0 + 128], plane[:, at0:at0 + 128], T.xb[:, 512 * h:512 * h + 512], free=True, on="s7")

    tt(T.ux[B0], T.ulf[B0], T.btr[B0], A.add, on="s5", after=[ku, ("m1", 24), last("dbo")])
    kso = fill(T.s2[:, 512:640], 0.0, on="sf")
    fill(T.rs7[:], 1.0, on="sz")
    ready = [ts(T.ul[B0], T.ux[B0], 0.5, A.mult, -0.25, A.add, on="s5", after=[kul]), last("drow")]
    ko2 = cp(T.off2[:], T.io32[:], free=True, on="*")
    fill(T.rs7[:, 0:112:7], 0.0, free=False, on="sz")
    keven = ts(new("even"), p, 16.0, A.is_lt, free=True, on="*")
    kgb = act(T.g2[:, 256:512], T.win[:].indirect(T.ul[:, 16:32]), C.Copy, on="sa", after=ready)
    kvs1 = act(T.vs1[:], T.io256[:].indirect(qsel), C.Copy, free=True, on="*", after=[kq])
    kc0 = act(T.c0m[:], T.vs1[:], scale=e2(N0), bias=T.bs[:, me:me + 1], on="*", after=[kvs1, kw2])
    cp(T.g2[:, 0:256], T.win[:].indirect(T.ul[:, 0:16]), on="sx", after=ready)
    kpk = cp(words(T.pk1[:]), words(T.pk0[:]).indirect(T.list1[:, 0:9]), after=[kp0])
    to_rest([ksc, last("drow"), last("dbo")], 0, s.f1s, lambda k: T.ps1[:, CAP * k:CAP * k + CAP], T.fs1[:])
    to_peer([ksc], s.c1, lambda k: T.ps1[:, CAP * k:CAP * k + CAP], T.cbs[:, CAP * at:CAP * at + CAP])
    to_rest([kpk], 0, s.f1c, lambda k: raw(T.pk1[:, CAP * k:CAP * k + CAP]), raw(T.fc1[:]))
    to_peer([kpk], s.c1, lambda k: raw(T.pk1[:, CAP * k:CAP * k + CAP]), raw(T.cb[:, CAP * at:CAP * at + CAP]))
    ks = scan(T.s2[:, 0:512], T.data0[:], T.g2[:], c("init2"), on="sx", after=[kgb, kw2, kd0, last("se")])
    for n, r in enumerate(others):
        kvsel = act(T.vsel[:, 64 * r:64 * r + 64], T.s2[:].indirect(T.offsel[:, 4 * r:4 * r + 4]), bias=T.bs[:, r:r + 1], free=n > 0, on="sa", after=[ks, kso])
    kq2 = quant(2)
    turn(T.tg2[B0], T.s2[B0, 0:512], on="sx")
    tt(T.vsel[:, 64 * me:64 * me + 64], T.s2[:].indirect(T.offsel[:, 4 * me:4 * me + 4]), T.c0m[:], A.add, free=True, on="so", after=[kso, kc0])
    for k in range(3):
        tt(T.x2[B0, k:112:7], T.tg2[B0, :, SENT + k], T.tg2[B0, :, GOES + k], A.mult, free=k > 0, on="sx")
    tt(T.x2[B0, 3:112:7], T.tg2[B0, :, PLACE], T.tg2[B0, :, ENDS], A.mult, free=True, on="sx")
    tt(T.x2[B0, 4:112:7], T.tg2[B0, :, ENDS], T.ntr[B0], A.mult, free=True, on="sx", after=[("g3", 2)])
    tt(T.x2[B0, 5:112:7], T.tg2[B0, :, LEAVES], T.ntr[B0], A.mult, free=True, on="sx")
    again(T.cb, T.cbs, LAND, 0)
    scan(T.y2[B0], T.rs7[B0], T.x2[B0], 0.0, on="sx", after=[last("sz")])
    kq1 = quant(1)
    ts(T.off2[B0], T.y2[B0, 6:112:7], float(M), A.add, on="sx", after=[ko2])
    kcb = again(T.cb, T.cbs, LAND + 128, 1)
    kw = cp(T.w2[:].indirect(T.off2[:]), T.vsel[:], on="sx", after=[last("so"), kvsel, ("g4", 1)])
    kwq = quant(0)
    wait(v, "v", *kw)

    def w(k):
        return T.wq[:, 128 * k:128 * k + 128], T.ws[:, 128 * k:128 * k + 128]
    m2 = mm(T.ps[:, 1024:1280], *w(2), T.xq[:], T.xs[:], True, True, free=True, after=[kq2, kxq])
    m1 = mm(T.ps[:, 512:768], *w(1), T.xq[:], T.xs[:], True, True, after=[kq1])
    m0 = mm(T.ps[:, 0:400], *w(0), T.cb[:], T.cbs[:], True, True, after=[kwq, ("c1", 48), kcb])
    for x, at0 in ((T.aw, LAND), (T.bw, 0), (T.cw, 0)):
        level(x[:, at0:at0 + 1], 0.0, free=True, on="sb")
    act(new("idb"), c("even"), C.Copy, scale=-1.0, free=True, on="sb", after=[keven])
    act(new("s2"), e2(SLOT), bias=e2(SLOT + 1), free=True, on="s3")
    act(new("u3"), p, scale=float(CAP), bias=-1.0 - LAND - CAP * SLOT, free=True, on="s3")
    act(new("s3"), e2(SLOT + 2), bias=c("s2"), on="s3")
    act(new("init3"), c("u3"), C.Copy, scale=c("even"), free=True, on="s3")
    k3 = level(T.data3[:], c("s3"), on="s3")
    act(T.cw[:, 1:257], T.ps[:, 1024:1280], C.Copy, free=True, on="sb", after=[m2])
    kbw = act(T.bw[:, 1:257], T.ps[:, 512:768], C.Copy, free=True, on="sb", after=[m1])
    kid = act(T.idl[:], T.w2[:, 0:M], bias=c("idb"), on="sk", after=[kw, kbw])
    dma(g.sync, T.id[:], T.idl[ID0:ID0 + 2, :], "did", after=[kid])

    cp(T.d2[B0, 0:18:2, :], T.w2[B0, M:M + LAND])
    cp(T.d2[B0, 1:18:2, :], T.w2[B0, M:M + LAND], free=True)
    scan(T.w3[B0], T.data3[B0], T.w2[B0, 0:M], c("init3")[B0], free=True, on="sd", after=[k3])
    turn(T.td2[B0], T.d2[B0])
    cp(T.dp[B0, 0:24:2, :], T.w3[B0], on="sd")
    cp(T.dp[B0, 1:24:2, :], T.w3[B0], free=True, on="sd")
    for b in range(2):
        for h, r in enumerate((N0, C1)):
            tt(T.nf[32 * b:32 * b + 32, :, h, :], T.td2[B0, :, :, r], T.td2[B0, :, :, TWIN + r], A.add, free=b + h > 0)
    turn(T.tp[B0], T.dp[B0], on="sd")
    for b in range(2):
        kl2 = ts(T.list2[64 * b:64 * b + 64], T.nf[0:64], LAND - 1.0, A.add, free=b > 0)
    tt(T.qz[B0, 0:12], T.tp[B0, :, C1], T.tp[B0, :, TWIN + C1], A.add, on="sd")
    tt(T.qz[B0, 12:24], T.tp[B0, :, C2], T.tp[B0, :, C2 + 1], A.add, free=True, on="sd")
    landed = [("c1", 48), kcb]
    ksa = act(T.ps2[:, 0:192], T.cbs[:].indirect(T.list2[:, 0:12]), C.Copy, on="sa", after=[kl2] + landed)
    ksb = act(T.ps2[:, 192:288], T.cbs[:].indirect(T.list2[:, 12:18]), C.Copy, on="*")
    kpa = cp(words(T.pk2[:, 0:192]), words(T.cb[:]).indirect(T.list2[:, 0:12]), after=landed)
    kpb = cp(words(T.pk2[:, 192:288]), words(T.cb[:]).indirect(T.list2[:, 12:18]), free=True, on="so")
    to_rest([kpa], 0, s.f2c, lambda k: raw(T.pk2[:, 96 * k:96 * k + 96]), raw(T.fc2[:]))
    to_rest([ksa], 0, s.f2s, lambda k: T.ps2[:, 96 * k:96 * k + 96], T.fs2[:])
    to_peer([kpb], s.c2p, lambda k: raw(T.pk2[:, 96 * k:96 * k + 96]), raw(T.lp[:, 0:96]))
    to_peer([ksb], s.c2p, lambda k: T.ps2[:, 96 * k:96 * k + 96], T.lps[:, 0:96])
    g.wait_ge(s.did, 16)
    g.dma_start(T.id[:], T.idl[TWIN + ID0:TWIN + ID0 + 2, :], accum_op=A.add).then_inc(s.dia, 16)

    tt(T.z3[B0], T.tp[B0, :, N0], T.tp[B0, :, TWIN + N0], A.add, free=True, on="sd")
    tt(T.fl[B0, :, 0:3], T.tp[B0, :, ON:ON + 3], T.tp[B0, :, TWIN + ON:TWIN + ON + 3], A.add, free=True, on="sd")
    tt(T.x3[B0, :, 0:3], T.tp[B0, :, SLOT:SLOT + 3], T.tp[B0, :, TWIN + SLOT:TWIN + SLOT + 3], A.add, free=True, on="sd")
    fill(T.rs[:], 1.0, on="sz")
    klp = vec(v.quantize_mx, T.lp[:, 96:224], T.lps[:, 96:224], T.xb[:, 0:512], free=True, on="*")
    ts(T.fl[B0, :, 3], T.qz[B0, 0:12], 1.0, A.min, on="sd")
    ts(T.x3[B0, :, 3], T.z3[B0], float(LAND), A.add, free=True, on="sd")
    for b in range(0, 128, 32):
        kqbc = cp(T.qbc[b:b + 32], T.qz[B0], free=True, on="sc")
    tt(T.x3m[B0], T.x3[B0], T.fl[B0], A.mult, on="sd")
    fill(T.rs[:, 0:48:4], 0.0, free=False, on="sz")
    kaw = act(T.aw[:, LAND + 1:LAND + 401], T.ps[:, 0:400], C.Copy, free=True, on="sb", after=[m0])
    kt1 = act(T.t1[:], T.cw[:, 0:257].indirect(T.qbc[:, 12:24]), C.Copy, on="sa", after=[kqbc, kbw])
    scan(T.y4[B0], T.rs[B0], T.x3m[B0], 0.0, on="sd", after=[last("sz")])
    for b in range(0, 128, 32):
        kq0 = ts(T.q0[b:b + 32], T.y4[B0, 3:48:4], float(LAND), A.add, free=b > 0, on="sd")
    tt(T.t2[:], T.bw[:, 0:257].indirect(T.qbc[:, 0:12]), T.t1[:], A.add, on="so", after=[kqbc, kt1])

    mm(T.ps[:, 2048:2176], *w(0), T.lp[:, 0:128], T.lps[:, 0:128], True, False, after=[klp, ("c2p", 16)])
    mp = mm(T.ps[:, 2048:2176], *w(1), T.lp[:, 48:176], T.lps[:, 48:176], False, True, free=True)
    mm(T.ps[:, 1536:1680], *w(0), T.lr[:, 0:144], T.lrs[:, 0:144], True, False, after=[("c2", 32)])
    mr = mm(T.ps[:, 1536:1680], *w(1), T.lr[:, 48:192], T.lrs[:, 48:192], False, True, free=True)
    kpw = act(T.aw[:, 96:144], T.ps[:, 2048:2096], C.Copy, free=True, on="sb", after=[mp])
    for k in rest:
        cp(T.aw[:, CAP * k:CAP * k + CAP], T.ps[:, 1536 + 96 * k:1536 + 96 * k + CAP], free=True, on="so", after=[mr])
    ky = tt(T.yo[:], T.aw[:, 0:LAND + 401].indirect(T.q0[:]), T.t2[:], A.add, on="so", after=[kq0, kpw])
    dma(g.sync, T.y[:], T.yo[:], "dy", after=[ky])

    g.wait_ge(s.dia, 16)
    for x in CHAINS + ["loc", "dy"]:
        if max([n for (q, y), n in known.items() if y == x] + [0]) < cnt.get(x, 0):
            wait(g, "g", x, cnt[x])
